import numpy as np
import ml_dtypes


def mxq(x, axis, fmt="e4m3"):
    dtype, down = {"e4m3": (ml_dtypes.float8_e4m3fn, 7), "e5m2": (ml_dtypes.float8_e5m2, 14)}[fmt]
    v = np.moveaxis(np.asarray(x, np.float32).astype(ml_dtypes.bfloat16).astype(np.float64), axis, -1)
    blocks = v.reshape(v.shape[:-1] + (-1, 32))
    amax = np.abs(blocks).max(-1, keepdims=True)
    byte = np.maximum(np.where(amax > 0, np.frexp(amax)[1] - 1 + 127, 0) - down, 1)
    scale = np.exp2(byte - 127.0)
    codes = (blocks / scale).astype(np.float32).astype(dtype).astype(np.float64)
    return np.moveaxis((codes * scale).reshape(v.shape), -1, axis)


WIDE = False


def mx_kscale(k):
    if not WIDE:
        return np.ones(k)
    levels = np.array([10, -10, 5, -5, 0])
    if k % 512:
        return np.exp2(np.random.permutation(np.resize(levels, k // 32))).repeat(32)
    a = np.empty((k // 512, 16))
    for p in range(k // 512):
        a[p, :8] = np.random.permutation(np.resize(levels, 8))
        for g in range(8):
            far = levels[np.abs(levels - a[p, g]) >= 10]
            a[p, g + 8] = far[np.random.randint(len(far))]
    return np.exp2(a.ravel()).repeat(32)


def f64(x):
    return np.asarray(x).astype(np.float64)


def striped(idx):
    return np.tile(idx.reshape(-1, 16).T, (8, 1)).astype(np.uint16)


def unstriped(offs):
    return offs[:16].T.reshape(-1).astype(np.int64)


E2M1 = np.array([0.0, 0.5, 1.0, 1.5, 2.0, 3.0, 4.0, 6.0, -0.0, -0.5, -1.0, -1.5, -2.0, -3.0, -4.0, -6.0])


def pack_weight(w, fmt):
    k, n = w.shape
    w = f64(np.asarray(w, np.float32).astype(ml_dtypes.bfloat16)).reshape(k // 32, 32, n)
    amax = np.abs(w).max(1)
    if fmt == "e4m3":
        byte = np.frexp(amax)[1] - 1 + 127 - 7
    else:
        mant, ex = np.frexp(amax / 6.0)
        byte = np.where(mant > 0.5, ex, ex - 1) + 127
    byte = np.clip(np.where(amax > 0, byte, 1), 1, 254)
    scaled = (w * np.exp2(127.0 - byte)[:, None, :]).reshape(k, n).astype(np.float32)
    by_word = np.ascontiguousarray(scaled.reshape(k // 512, 128, 4, n).transpose(0, 1, 3, 2))
    if fmt == "e4m3":
        words = by_word.astype(ml_dtypes.float8_e4m3fn).view(np.uint8)
    else:
        c = by_word.astype(ml_dtypes.float4_e2m1fn).view(np.uint8) & 0xF
        words = (c[..., 0::2] | (c[..., 1::2] << 4)).reshape(k // 512, 128, 2 * n)
    return np.ascontiguousarray(words), np.ascontiguousarray(byte.astype(np.uint8).reshape(k // 512, 16, n))


def unpack_weight(words, scales, fmt):
    g, _, n = scales.shape
    words = np.ascontiguousarray(words).reshape(g, 128, n, -1)
    if fmt == "e4m3":
        vals = words.view(ml_dtypes.float8_e4m3fn).astype(np.float64)
    else:
        nib = np.empty((g, 128, n, 4), np.uint8)
        nib[..., 0::2] = words & 0xF
        nib[..., 1::2] = words >> 4
        vals = E2M1[nib]
    vals = vals * np.repeat(np.exp2(scales.astype(np.float64) - 127.0), 8, axis=1)[..., None]
    return vals.transpose(0, 1, 3, 2).reshape(g * 512, n)


def gelu(v):
    return 0.5 * v * (1.0 + np.tanh(np.sqrt(2.0 / np.pi) * (v + 0.044715 * v**3)))


K, T, S, H, N = 1024, 2048, 1024, 1024, 256

def setup_inputs():
    n = np.random.standard_normal
    s = mx_kscale(K)[:, None]
    u = mx_kscale(H)[:, None]
    tab_words, tab_scales = pack_weight(n((K, T)) * s, "e4m3")
    wb_words, wb_scales = pack_weight(n((K, H)) / np.sqrt(K) / s * u.T, "e2m1")
    return {
        "tab_words": tab_words, "tab_scales": tab_scales,
        "offs": striped(np.random.permutation(T)[:S]),
        "wa": (n((K, H)) / np.sqrt(K) / s * u.T).astype(np.float32),
        "wb_words": wb_words, "wb_scales": wb_scales,
        "gT": (0.8 * n((H, T))).astype(np.float32),
        "drift": (0.5 * n(H) * u[:, 0]).astype(np.float32),
        "wc": (n((H, N)) / np.sqrt(H) / u).astype(np.float32),
        "xop": (0.5 * n(N)).astype(np.float32),
    }

def reference(tab_words, tab_scales, offs, wa, wb_words, wb_scales, gT, drift, wc, xop):
    v = unpack_weight(tab_words, tab_scales, "e4m3")[:, unstriped(offs)]
    g = f64(gT)[:, unstriped(offs)]
    a = mxq(f64(wa), 0, "e4m3").T @ v
    b = unpack_weight(wb_words, wb_scales, "e2m1").T @ v
    h = a + g * b + f64(drift)[:, None]
    y = mxq(f64(wc), 0, "e4m3").T @ mxq(h, 0, "e4m3")
    return y + f64(xop)[:, None]

@@ -1,0 +1,294 @@
+from contextlib import ExitStack
+
+import concourse.mybir as mybir
+
+K, T, S, H, N = 1024, 2048, 1024, 1024, 256
+FLOPS = 2 * K * H * S * 2 + 2 * H * N * S
+
+F32 = mybir.dt.float32
+BF16 = mybir.dt.bfloat16
+I32 = mybir.dt.int32
+U32 = mybir.dt.uint32
+U16 = mybir.dt.uint16
+U8 = mybir.dt.uint8
+FP8X4 = mybir.dt.float8_e4m3fn_x4
+FP4X4 = mybir.dt.float4_e2m1fn_x4
+IDENT = mybir.ActivationFunctionType.Identity
+MULT = mybir.AluOpType.mult
+ADD = mybir.AluOpType.add
+
+P = 128
+PACK = 4
+KP = P * PACK
+HALF = 512
+RUN = 4
+HALVES = [(0, 512), (512, 1024)]
+TAIL = [(0, 512), (512, 768), (768, 1024)]
+
+
+def tile_list_bilinear_koopman_step_kernel(
+    tc, tab_words, tab_scales, offs, wa, wb_words, wb_scales, gT, drift, wc, xop, out
+):
+    nc = tc.nc
+    with ExitStack() as ctx:
+        keep = ctx.enter_context(tc.tile_pool(name="keep", bufs=1))
+        slab = ctx.enter_context(tc.tile_pool(name="slab", bufs=10))
+        stage = ctx.enter_context(tc.tile_pool(name="stage", bufs=2))
+        bpool = ctx.enter_context(tc.tile_pool(name="bpool", bufs=4))
+        apool = ctx.enter_context(tc.tile_pool(name="apool", bufs=3))
+        psum = ctx.enter_context(tc.psum_pool(name="psum", bufs=8))
+
+        offsets = keep.tile([P, S // 16], U16, name="offsets")
+        tsc = [keep.tile([P, 1, T], U8, name=f"tsc{a}", align_bytes=64) for a in range(2)]
+        wbs_raw = keep.tile([P, 2, H], U8, name="wbs_raw", align_bytes=64)
+        wbw_raw = [keep.tile([P, 2, 2 * KP], U8, name=f"wbw_raw{b}", align_bytes=64) for b in range(2)]
+        wbw = [keep.tile([P, PACK, 2, 2 * P], U8, name=f"wbw{b}", align_bytes=64) for b in range(2)]
+        wbs = [keep.tile([P, PACK, 2, P], U8, name=f"wbs{b}", align_bytes=64) for b in range(2)]
+        vw = [keep.tile([P, S], U32, name=f"vw{a}", align_bytes=64) for a in range(2)]
+        vs = [keep.tile([P, S], U8, name=f"vs{a}", align_bytes=64) for a in range(2)]
+        waw = [[keep.tile([P, KP], U32, name=f"waw{b}{a}", align_bytes=64) for a in range(2)] for b in range(2)]
+        was = [[keep.tile([P, KP], U8, name=f"was{b}{a}", align_bytes=64) for a in range(2)] for b in range(2)]
+        wcw = keep.tile([P, 2, N], U32, name="wcw", align_bytes=64)
+        wcs = keep.tile([P, 2, N], U8, name="wcs", align_bytes=64)
+        hw = [keep.tile([P, S], U32, name=f"hw{b}", align_bytes=64) for b in range(2)]
+        hs = [keep.tile([P, S], U8, name=f"hs{b}", align_bytes=64) for b in range(2)]
+        gb = [keep.tile([P, PACK, S], F32, name=f"gb{b}") for b in range(2)]
+        drift_col = [[keep.tile([P, 1], F32, name=f"drift{b}{t}") for t in range(PACK)] for b in range(2)]
+        xop_col = keep.tile([P, 2], F32, name="xop_col")
+
+        def load_table_words(a):
+            tile = slab.tile([P, T], I32, name="slab")
+            nc.sync.dma_start(tile[:], tab_words[a].rearrange("p t i -> p (t i)").bitcast(I32))
+            return tile
+
+        def load_g(b, t):
+            tile = slab.tile([P, T], F32, name="slab")
+            rows = gT[b * KP : (b + 1) * KP, :].rearrange("(q t e) c -> t q e c", t=PACK, e=RUN)
+            nc.sync.dma_start(tile[:], rows[t])
+            return tile
+
+        def load_wa(b, a):
+            tile = slab.tile([P, PACK, KP], F32, name="slab")
+            rows = wa[a * KP : (a + 1) * KP, b * KP : (b + 1) * KP]
+            nc.sync.dma_start(tile[:], rows.rearrange("(p j) c -> p j c", j=PACK))
+            return tile
+
+        def load_wc():
+            tile = slab.tile([P, 2, PACK, N], F32, name="slab")
+            rows = wc.rearrange("(b q t e) n -> b t q e n", b=2, t=PACK, e=RUN)
+            for b in range(2):
+                for t in range(PACK):
+                    nc.sync.dma_start(tile[:, b, t, :], rows[b, t])
+            return tile
+
+        def load_drift(b, t):
+            vals = drift.rearrange("(b q t e u) -> b t q e u", b=2, t=PACK, e=RUN, u=1)
+            with nc.allow_non_contiguous_dma(reason="one bias value a partition"):
+                nc.sync.dma_start(drift_col[b][t][:], vals[b, t])
+
+        def load_wb_words(b):
+            src = wb_words[:, :, b * 2 * KP : (b + 1) * 2 * KP].rearrange("a p c -> p a c")
+            nc.sync.dma_start(wbw_raw[b][:].bitcast(I32), src.bitcast(I32))
+
+        def load_scales(tile, src):
+            for q in range(4):
+                rows = src[:, 4 * q : 4 * q + 4, :].rearrange("a r c -> r a c")
+                nc.sync.dma_start(tile[32 * q : 32 * q + 4, :, :].bitcast(I32), rows.bitcast(I32))
+
+        def listed(lo, hi):
+            return offsets[:, lo // 16 : hi // 16]
+
+        def gather_scales(a, lo, hi):
+            nc.vector.tensor_copy(vs[a][:, lo:hi], tsc[a][:, 0, :].indirect(listed(lo, hi)))
+
+        def gather_words(a, window, lo, hi):
+            nc.vector.tensor_copy(vw[a][:, lo:hi], window[:].bitcast(U32).indirect(listed(lo, hi)))
+
+        def permute_wb(b):
+            nc.vector.tensor_copy(
+                wbw[b][:].rearrange("p t a c -> p t (a c)").bitcast(I32).rearrange("p t (x w) -> p t x w", w=2),
+                wbw_raw[b][:].rearrange("p a c -> p (a c)").bitcast(I32).rearrange("p (x t w) -> p t x w", t=PACK, w=2),
+            )
+            nc.vector.tensor_copy(
+                wbs[b][:].bitcast(I32),
+                wbs_raw[:, :, b * KP : (b + 1) * KP].bitcast(I32).rearrange("p a (q t) -> p t a q", t=PACK),
+            )
+
+        def cast_wa(raw):
+            tile = stage.tile([P, PACK, KP], BF16, name="wa_bf", align_bytes=64)
+            cols = raw[:].rearrange("p j (q t e) -> p t q j e", t=PACK, e=RUN)
+            for t in range(PACK):
+                nc.scalar.copy(tile[:, t, :].rearrange("p (q e j) -> p q j e", e=RUN, j=PACK), cols[:, t])
+            return tile
+
+        def quant_wa(b, a, tile):
+            nc.vector.quantize_mx(out=waw[b][a][:].bitcast(FP8X4), scales=was[b][a][:], in_=tile[:].rearrange("p t c -> p (t c)"))
+
+        def product_b(b, t):
+            b_sb = bpool.tile([P, S], F32, name="b_sb")
+            for lo, hi in HALVES:
+                acc = psum.tile([P, HALF], F32, name="acc")
+                for a in range(2):
+                    nc.tensor.matmul_mx(
+                        out=acc[:],
+                        lhsT=wbw[b][:, t, a, :].bitcast(FP4X4),
+                        lhsT_scale=wbs[b][:, t, a, :],
+                        rhs=vw[a][:, lo:hi].bitcast(FP8X4),
+                        rhs_scale=vs[a][:, lo:hi],
+                        start=(a == 0),
+                        stop=(a == 1),
+                    )
+                nc.scalar.copy(b_sb[:, lo:hi], acc[:])
+            return b_sb
+
+        def product_a(b, lo, hi):
+            a_sb = apool.tile([P, PACK, HALF], F32, name="a_sb")
+            for t in range(PACK):
+                acc = psum.tile([P, HALF], F32, name="acc")
+                for a in range(2):
+                    nc.tensor.matmul_mx(
+                        out=acc[:],
+                        lhsT=waw[b][a][:, P * t : P * (t + 1)].bitcast(FP8X4),
+                        lhsT_scale=was[b][a][:, P * t : P * (t + 1)],
+                        rhs=vw[a][:, lo:hi].bitcast(FP8X4),
+                        rhs_scale=vs[a][:, lo:hi],
+                        start=(a == 0),
+                        stop=(a == 1),
+                    )
+                nc.scalar.activation(a_sb[:, t, :], acc[:], IDENT, bias=drift_col[b][t][:])
+            return a_sb
+
+        def gate(b, t, window, b_sb, lo, hi):
+            nc.vector.tensor_tensor(gb[b][:, t, lo:hi], window[:].indirect(listed(lo, hi)), b_sb[:, lo:hi], MULT)
+
+        def add_h(b, a_sb, lo, hi):
+            tile = stage.tile([P, PACK * (hi - lo)], BF16, name="h_bf", align_bytes=64)
+            base = lo % HALF
+            nc.vector.tensor_tensor(
+                tile[:].rearrange("p (c i t) -> p c t i", i=2, t=PACK),
+                a_sb[:, :, base : base + hi - lo].rearrange("p t (c i) -> p c t i", i=2),
+                gb[b][:, :, lo:hi].rearrange("p t (c i) -> p c t i", i=2),
+                ADD,
+            )
+            return tile
+
+        def quant_h(b, tile, lo, hi):
+            nc.vector.quantize_mx(out=hw[b][:, lo:hi].bitcast(FP8X4), scales=hs[b][:, lo:hi], in_=tile[:])
+
+        def decode(lo, hi, share):
+            res = stage.tile([P, 2, hi - lo], F32, name="res", bufs=3)
+            for c in range(2):
+                acc = psum.tile([P, hi - lo], F32, name="acc")
+                for b in range(2):
+                    nc.tensor.matmul_mx(
+                        out=acc[:],
+                        lhsT=wcw[:, b, P * c : P * (c + 1)].bitcast(FP8X4),
+                        lhsT_scale=wcs[:, b, P * c : P * (c + 1)],
+                        rhs=hw[b][:, lo:hi].bitcast(FP8X4),
+                        rhs_scale=hs[b][:, lo:hi],
+                        start=(b == 0),
+                        stop=(b == 1),
+                    )
+                if share and c == 1:
+                    nc.vector.tensor_scalar_add(res[:, c, :], acc[:], xop_col[:, c : c + 1])
+                else:
+                    nc.scalar.activation(res[:, c, :], acc[:], IDENT, bias=xop_col[:, c : c + 1])
+            nc.sync.dma_start(out[:, lo:hi].rearrange("(c p) j -> p c j", p=P), res[:])
+
+        nc.vector.memset(tsc[1][:].bitcast(I32), 0)
+        nc.gpsimd.memset(wbs_raw[:].bitcast(I32), 0)
+        nc.sync.dma_start(offsets[:], offs)
+        for q in range(4):
+            rows = tab_scales[0, 4 * q : 4 * q + 4, :].bitcast(I32)
+            nc.sync.dma_start(tsc[0][32 * q : 32 * q + 32, 0, :].bitcast(I32), rows.unsqueeze(0).broadcast_to([8, 4, T // 4]))
+        tw = [load_table_words(a) for a in range(2)]
+        load_wb_words(0)
+        load_scales(tsc[1], tab_scales[1:2])
+        g = {}
+        wa_raw = {}
+        g[0, 0] = load_g(0, 0)
+        load_scales(wbs_raw, wb_scales)
+        wa_raw[0, 0] = load_wa(0, 0)
+        load_drift(0, 0)
+        g[0, 1] = load_g(0, 1)
+        load_drift(0, 1)
+        wa_raw[0, 1] = load_wa(0, 1)
+        load_drift(0, 2)
+        g[0, 2] = load_g(0, 2)
+        load_drift(0, 3)
+        g[0, 3] = load_g(0, 3)
+        load_wb_words(1)
+        g[1, 0] = load_g(1, 0)
+        load_drift(1, 0)
+        wa_raw[1, 0] = load_wa(1, 0)
+        load_drift(1, 1)
+
+        gather_scales(0, 0, S)
+        gather_words(0, tw[0], 0, S)
+        gather_words(1, tw[1], 0, S)
+        permute_wb(0)
+        for lo, hi in HALVES:
+            gather_scales(1, lo, hi)
+        wa_raw[1, 1] = load_wa(1, 1)
+        load_drift(1, 2)
+        g[1, 1] = load_g(1, 1)
+        load_drift(1, 3)
+
+        b_sb = product_b(0, 0)
+        for lo, hi in HALVES:
+            gate(0, 0, g[0, 0], b_sb, lo, hi)
+        g[1, 2] = load_g(1, 2)
+        b_sb = product_b(0, 1)
+        wa_bf = cast_wa(wa_raw[0, 0])
+        gate(0, 1, g[0, 1], b_sb, 0, S)
+        quant_wa(0, 0, wa_bf)
+        with nc.allow_non_contiguous_dma(reason="one bias value a partition"):
+            nc.sync.dma_start(xop_col[:], xop.rearrange("(c p) -> p c", p=P))
+        g[1, 3] = load_g(1, 3)
+        wc_raw = load_wc()
+        b_sb = product_b(0, 2)
+        wa_bf = cast_wa(wa_raw[0, 1])
+        gate(0, 2, g[0, 2], b_sb, 0, S)
+        quant_wa(0, 1, wa_bf)
+        b_sb = product_b(0, 3)
+        a_sb = [product_a(0, lo, hi) for lo, hi in HALVES]
+        gate(0, 3, g[0, 3], b_sb, 0, S)
+        permute_wb(1)
+        h_bf = [add_h(0, a_sb[u], lo, hi) for u, (lo, hi) in enumerate(HALVES)]
+        b_next = product_b(1, 0)
+        for u, (lo, hi) in enumerate(HALVES):
+            quant_h(0, h_bf[u], lo, hi)
+
+        wa_bf = cast_wa(wa_raw[1, 0])
+        gate(1, 0, g[1, 0], b_next, 0, S)
+        quant_wa(1, 0, wa_bf)
+        b_sb = product_b(1, 1)
+        wa_bf = cast_wa(wa_raw[1, 1])
+        gate(1, 1, g[1, 1], b_sb, 0, S)
+        quant_wa(1, 1, wa_bf)
+        b_sb = product_b(1, 2)
+        b_last = product_b(1, 3)
+        a_sb = [product_a(1, lo, hi) for lo, hi in HALVES]
+        gate(1, 2, g[1, 2], b_sb, 0, S)
+        wc_bf = keep.tile([P, 2, PACK * N], BF16, name="wc_bf", align_bytes=64)
+        for b in range(2):
+            nc.scalar.copy(
+                wc_bf[:, b, :].rearrange("p (c i t) -> p c t i", i=2, t=PACK),
+                wc_raw[:, b].rearrange("p t (c i) -> p c t i", i=2),
+            )
+        for lo, hi in HALVES:
+            gate(1, 3, g[1, 3], b_last, lo, hi)
+        nc.vector.quantize_mx(
+            out=wcw[:].rearrange("p b n -> p (b n)").bitcast(FP8X4),
+            scales=wcs[:].rearrange("p b n -> p (b n)"),
+            in_=wc_bf[:].rearrange("p b n -> p (b n)"),
+        )
+        pending = None
+        for lo, hi in TAIL:
+            tile = add_h(1, a_sb[lo // HALF], lo, hi)
+            if pending is not None:
+                quant_h(1, *pending)
+                decode(pending[1], pending[2], False)
+            pending = (tile, lo, hi)
+        quant_h(1, *pending)
+        decode(pending[1], pending[2], True)

@@ -21,7 +21,6 @@ P = 128
 PACK = 4
 KP = P * PACK
 HALF = 512
-RUN = 4
 HALVES = [(0, 512), (512, 1024)]
 TAIL = [(0, 512), (512, 768), (768, 1024)]
 
@@ -33,27 +32,30 @@ def tile_list_bilinear_koopman_step_kernel(
     with ExitStack() as ctx:
         keep = ctx.enter_context(tc.tile_pool(name="keep", bufs=1))
         slab = ctx.enter_context(tc.tile_pool(name="slab", bufs=10))
-        stage = ctx.enter_context(tc.tile_pool(name="stage", bufs=2))
         bpool = ctx.enter_context(tc.tile_pool(name="bpool", bufs=4))
-        apool = ctx.enter_context(tc.tile_pool(name="apool", bufs=3))
         psum = ctx.enter_context(tc.psum_pool(name="psum", bufs=8))
 
         offsets = keep.tile([P, S // 16], U16, name="offsets")
         tsc = [keep.tile([P, 1, T], U8, name=f"tsc{a}", align_bytes=64) for a in range(2)]
         wbs_raw = keep.tile([P, 2, H], U8, name="wbs_raw", align_bytes=64)
-        wbw_raw = [keep.tile([P, 2, 2 * KP], U8, name=f"wbw_raw{b}", align_bytes=64) for b in range(2)]
-        wbw = [keep.tile([P, PACK, 2, 2 * P], U8, name=f"wbw{b}", align_bytes=64) for b in range(2)]
-        wbs = [keep.tile([P, PACK, 2, P], U8, name=f"wbs{b}", align_bytes=64) for b in range(2)]
+        wbw_raw = keep.tile([P, 2, 2 * H], U8, name="wbw_raw", align_bytes=64)
+        wbw = keep.tile([P, PACK, 2, 2, 2 * P], U8, name="wbw", align_bytes=64)
+        wbs = keep.tile([P, PACK, 2, 2, P], U8, name="wbs", align_bytes=64)
         vw = [keep.tile([P, S], U32, name=f"vw{a}", align_bytes=64) for a in range(2)]
         vs = [keep.tile([P, S], U8, name=f"vs{a}", align_bytes=64) for a in range(2)]
-        waw = [[keep.tile([P, KP], U32, name=f"waw{b}{a}", align_bytes=64) for a in range(2)] for b in range(2)]
-        was = [[keep.tile([P, KP], U8, name=f"was{b}{a}", align_bytes=64) for a in range(2)] for b in range(2)]
+        waw = [keep.tile([P, 2, KP], U32, name=f"waw{b}", align_bytes=64) for b in range(2)]
+        was = [keep.tile([P, 2, KP], U8, name=f"was{b}", align_bytes=64) for b in range(2)]
         wcw = keep.tile([P, 2, N], U32, name="wcw", align_bytes=64)
         wcs = keep.tile([P, 2, N], U8, name="wcs", align_bytes=64)
+        wc_bf = keep.tile([P, 2, PACK * N], BF16, name="wc_bf", align_bytes=64)
         hw = [keep.tile([P, S], U32, name=f"hw{b}", align_bytes=64) for b in range(2)]
         hs = [keep.tile([P, S], U8, name=f"hs{b}", align_bytes=64) for b in range(2)]
+        h_bf = [keep.tile([P, PACK * S], BF16, name=f"h_bf{b}", align_bytes=64) for b in range(2)]
         gb = [keep.tile([P, PACK, S], F32, name=f"gb{b}") for b in range(2)]
-        drift_col = [[keep.tile([P, 1], F32, name=f"drift{b}{t}") for t in range(PACK)] for b in range(2)]
+        wa_bf = keep.tile([P, 2, PACK * KP], BF16, name="wa_bf", align_bytes=64)
+        a_sb = keep.tile([P, PACK, S], F32, name="a_sb")
+        res = keep.tile([P, 2 * S], F32, name="res")
+        drift_col = keep.tile([P, 2, PACK], F32, name="drift_col")
         xop_col = keep.tile([P, 2], F32, name="xop_col")
 
         def load_table_words(a):
@@ -63,8 +65,8 @@ def tile_list_bilinear_koopman_step_kernel(
 
         def load_g(b, t):
             tile = slab.tile([P, T], F32, name="slab")
-            rows = gT[b * KP : (b + 1) * KP, :].rearrange("(q t e) c -> t q e c", t=PACK, e=RUN)
-            nc.sync.dma_start(tile[:], rows[t])
+            rows = gT[b * KP : (b + 1) * KP, :].rearrange("(p t) c -> p t c", t=PACK)
+            nc.sync.dma_start(tile[:], rows[:, t, :])
             return tile
 
         def load_wa(b, a):
@@ -74,21 +76,9 @@ def tile_list_bilinear_koopman_step_kernel(
             return tile
 
         def load_wc():
-            tile = slab.tile([P, 2, PACK, N], F32, name="slab")
-            rows = wc.rearrange("(b q t e) n -> b t q e n", b=2, t=PACK, e=RUN)
-            for b in range(2):
-                for t in range(PACK):
-                    nc.sync.dma_start(tile[:, b, t, :], rows[b, t])
+            tile = slab.tile([P, 2, PACK * N], F32, name="slab")
+            nc.sync.dma_start(tile[:], wc.rearrange("(b p t) n -> p b (t n)", b=2, t=PACK))
             return tile
-
-        def load_drift(b, t):
-            vals = drift.rearrange("(b q t e u) -> b t q e u", b=2, t=PACK, e=RUN, u=1)
-            with nc.allow_non_contiguous_dma(reason="one bias value a partition"):
-                nc.sync.dma_start(drift_col[b][t][:], vals[b, t])
-
-        def load_wb_words(b):
-            src = wb_words[:, :, b * 2 * KP : (b + 1) * 2 * KP].rearrange("a p c -> p a c")
-            nc.sync.dma_start(wbw_raw[b][:].bitcast(I32), src.bitcast(I32))
 
         def load_scales(tile, src):
             for q in range(4):
@@ -104,25 +94,28 @@ def tile_list_bilinear_koopman_step_kernel(
         def gather_words(a, window, lo, hi):
             nc.vector.tensor_copy(vw[a][:, lo:hi], window[:].bitcast(U32).indirect(listed(lo, hi)))
 
-        def permute_wb(b):
+        def permute_wb():
             nc.vector.tensor_copy(
-                wbw[b][:].rearrange("p t a c -> p t (a c)").bitcast(I32).rearrange("p t (x w) -> p t x w", w=2),
-                wbw_raw[b][:].rearrange("p a c -> p (a c)").bitcast(I32).rearrange("p (x t w) -> p t x w", t=PACK, w=2),
+                wbw[:].rearrange("p t a b c -> p t (a b c)").bitcast(U16),
+                wbw_raw[:].rearrange("p a c -> p (a c)").bitcast(U16).rearrange("p (x t) -> p t x", t=PACK),
             )
             nc.vector.tensor_copy(
-                wbs[b][:].bitcast(I32),
-                wbs_raw[:, :, b * KP : (b + 1) * KP].bitcast(I32).rearrange("p a (q t) -> p t a q", t=PACK),
+                wbs[:].rearrange("p t a b c -> p t (a b c)"),
+                wbs_raw[:].rearrange("p a (x t) -> p t (a x)", t=PACK),
             )
 
-        def cast_wa(raw):
-            tile = stage.tile([P, PACK, KP], BF16, name="wa_bf", align_bytes=64)
-            cols = raw[:].rearrange("p j (q t e) -> p t q j e", t=PACK, e=RUN)
-            for t in range(PACK):
-                nc.scalar.copy(tile[:, t, :].rearrange("p (q e j) -> p q j e", e=RUN, j=PACK), cols[:, t])
-            return tile
+        def cast_wa(a, raw):
+            dst = wa_bf[:, a, :].rearrange("p (s i m j) -> p s m j i", s=2, i=2, j=PACK)
+            src = raw[:].rearrange("p j (m s i) -> p s m j i", s=2, i=2)
+            for s in range(2):
+                nc.scalar.copy(dst[:, s], src[:, s])
 
-        def quant_wa(b, a, tile):
-            nc.vector.quantize_mx(out=waw[b][a][:].bitcast(FP8X4), scales=was[b][a][:], in_=tile[:].rearrange("p t c -> p (t c)"))
+        def quant_wa(b):
+            nc.vector.quantize_mx(
+                out=waw[b][:].rearrange("p a c -> p (a c)").bitcast(FP8X4),
+                scales=was[b][:].rearrange("p a c -> p (a c)"),
+                in_=wa_bf[:].rearrange("p a c -> p (a c)"),
+            )
 
         def product_b(b, t):
             b_sb = bpool.tile([P, S], F32, name="b_sb")
@@ -131,8 +124,8 @@ def tile_list_bilinear_koopman_step_kernel(
                 for a in range(2):
                     nc.tensor.matmul_mx(
                         out=acc[:],
-                        lhsT=wbw[b][:, t, a, :].bitcast(FP4X4),
-                        lhsT_scale=wbs[b][:, t, a, :],
+                        lhsT=wbw[:, t, a, b, :].bitcast(FP4X4),
+                        lhsT_scale=wbs[:, t, a, b, :],
                         rhs=vw[a][:, lo:hi].bitcast(FP8X4),
                         rhs_scale=vs[a][:, lo:hi],
                         start=(a == 0),
@@ -141,42 +134,47 @@ def tile_list_bilinear_koopman_step_kernel(
                 nc.scalar.copy(b_sb[:, lo:hi], acc[:])
             return b_sb
 
-        def product_a(b, lo, hi):
-            a_sb = apool.tile([P, PACK, HALF], F32, name="a_sb")
-            for t in range(PACK):
-                acc = psum.tile([P, HALF], F32, name="acc")
-                for a in range(2):
-                    nc.tensor.matmul_mx(
-                        out=acc[:],
-                        lhsT=waw[b][a][:, P * t : P * (t + 1)].bitcast(FP8X4),
-                        lhsT_scale=was[b][a][:, P * t : P * (t + 1)],
-                        rhs=vw[a][:, lo:hi].bitcast(FP8X4),
-                        rhs_scale=vs[a][:, lo:hi],
-                        start=(a == 0),
-                        stop=(a == 1),
-                    )
-                nc.scalar.activation(a_sb[:, t, :], acc[:], IDENT, bias=drift_col[b][t][:])
-            return a_sb
+        def product_a(b):
+            for lo, hi in HALVES:
+                for t in range(PACK):
+                    acc = psum.tile([P, HALF], F32, name="acc")
+                    for a in range(2):
+                        nc.tensor.matmul_mx(
+                            out=acc[:],
+                            lhsT=waw[b][:, a, P * t : P * (t + 1)].bitcast(FP8X4),
+                            lhsT_scale=was[b][:, a, P * t : P * (t + 1)],
+                            rhs=vw[a][:, lo:hi].bitcast(FP8X4),
+                            rhs_scale=vs[a][:, lo:hi],
+                            start=(a == 0),
+                            stop=(a == 1),
+                        )
+                    nc.scalar.activation(a_sb[:, t, lo:hi], acc[:], IDENT, bias=drift_col[:, b, t : t + 1])
 
-        def gate(b, t, window, b_sb, lo, hi):
-            nc.vector.tensor_tensor(gb[b][:, t, lo:hi], window[:].indirect(listed(lo, hi)), b_sb[:, lo:hi], MULT)
+        def gate(b, t, b_sb, lo, hi):
+            nc.vector.tensor_tensor(gb[b][:, t, lo:hi], g[b, t][:].indirect(listed(lo, hi)), b_sb[:, lo:hi], MULT)
 
-        def add_h(b, a_sb, lo, hi):
-            tile = stage.tile([P, PACK * (hi - lo)], BF16, name="h_bf", align_bytes=64)
-            base = lo % HALF
+        def add_h(b, lo, hi):
             nc.vector.tensor_tensor(
-                tile[:].rearrange("p (c i t) -> p c t i", i=2, t=PACK),
-                a_sb[:, :, base : base + hi - lo].rearrange("p t (c i) -> p c t i", i=2),
+                h_bf[b][:, PACK * lo : PACK * hi].rearrange("p (c i t) -> p c t i", i=2, t=PACK),
+                a_sb[:, :, lo:hi].rearrange("p t (c i) -> p c t i", i=2),
                 gb[b][:, :, lo:hi].rearrange("p t (c i) -> p c t i", i=2),
                 ADD,
             )
-            return tile
 
-        def quant_h(b, tile, lo, hi):
-            nc.vector.quantize_mx(out=hw[b][:, lo:hi].bitcast(FP8X4), scales=hs[b][:, lo:hi], in_=tile[:])
+        def quant_h(b, lo, hi):
+            nc.vector.quantize_mx(
+                out=hw[b][:, lo:hi].bitcast(FP8X4), scales=hs[b][:, lo:hi], in_=h_bf[b][:, PACK * lo : PACK * hi]
+            )
+
+        def quant_wc():
+            nc.vector.quantize_mx(
+                out=wcw[:].rearrange("p b n -> p (b n)").bitcast(FP8X4),
+                scales=wcs[:].rearrange("p b n -> p (b n)"),
+                in_=wc_bf[:].rearrange("p b n -> p (b n)"),
+            )
 
         def decode(lo, hi, share):
-            res = stage.tile([P, 2, hi - lo], F32, name="res", bufs=3)
+            piece = res[:, 2 * lo : 2 * hi].rearrange("p (c j) -> p c j", c=2)
             for c in range(2):
                 acc = psum.tile([P, hi - lo], F32, name="acc")
                 for b in range(2):
@@ -190,10 +188,10 @@ def tile_list_bilinear_koopman_step_kernel(
                         stop=(b == 1),
                     )
                 if share and c == 1:
-                    nc.vector.tensor_scalar_add(res[:, c, :], acc[:], xop_col[:, c : c + 1])
+                    nc.vector.tensor_scalar_add(piece[:, c, :], acc[:], xop_col[:, c : c + 1])
                 else:
-                    nc.scalar.activation(res[:, c, :], acc[:], IDENT, bias=xop_col[:, c : c + 1])
-            nc.sync.dma_start(out[:, lo:hi].rearrange("(c p) j -> p c j", p=P), res[:])
+                    nc.scalar.activation(piece[:, c, :], acc[:], IDENT, bias=xop_col[:, c : c + 1])
+            nc.sync.dma_start(out[:, lo:hi].rearrange("(c p) j -> p c j", p=P), piece)
 
         nc.vector.memset(tsc[1][:].bitcast(I32), 0)
         nc.gpsimd.memset(wbs_raw[:].bitcast(I32), 0)
@@ -202,93 +200,74 @@ def tile_list_bilinear_koopman_step_kernel(
             rows = tab_scales[0, 4 * q : 4 * q + 4, :].bitcast(I32)
             nc.sync.dma_start(tsc[0][32 * q : 32 * q + 32, 0, :].bitcast(I32), rows.unsqueeze(0).broadcast_to([8, 4, T // 4]))
         tw = [load_table_words(a) for a in range(2)]
-        load_wb_words(0)
+        nc.sync.dma_start(wbw_raw[:].bitcast(I32), wb_words.rearrange("a p c -> p a c").bitcast(I32))
         load_scales(tsc[1], tab_scales[1:2])
         g = {}
         wa_raw = {}
         g[0, 0] = load_g(0, 0)
         load_scales(wbs_raw, wb_scales)
         wa_raw[0, 0] = load_wa(0, 0)
-        load_drift(0, 0)
         g[0, 1] = load_g(0, 1)
-        load_drift(0, 1)
         wa_raw[0, 1] = load_wa(0, 1)
-        load_drift(0, 2)
+        nc.sync.dma_start(drift_col[:], drift.rearrange("(b p t) -> p b t", b=2, t=PACK))
         g[0, 2] = load_g(0, 2)
-        load_drift(0, 3)
         g[0, 3] = load_g(0, 3)
-        load_wb_words(1)
         g[1, 0] = load_g(1, 0)
-        load_drift(1, 0)
+        with nc.allow_non_contiguous_dma(reason="one bias value a partition"):
+            nc.sync.dma_start(xop_col[:], xop.rearrange("(c p) -> p c", p=P))
         wa_raw[1, 0] = load_wa(1, 0)
-        load_drift(1, 1)
 
         gather_scales(0, 0, S)
         gather_words(0, tw[0], 0, S)
         gather_words(1, tw[1], 0, S)
-        permute_wb(0)
+        permute_wb()
         for lo, hi in HALVES:
             gather_scales(1, lo, hi)
         wa_raw[1, 1] = load_wa(1, 1)
-        load_drift(1, 2)
         g[1, 1] = load_g(1, 1)
-        load_drift(1, 3)
 
         b_sb = product_b(0, 0)
         for lo, hi in HALVES:
-            gate(0, 0, g[0, 0], b_sb, lo, hi)
+            gate(0, 0, b_sb, lo, hi)
         g[1, 2] = load_g(1, 2)
         b_sb = product_b(0, 1)
-        wa_bf = cast_wa(wa_raw[0, 0])
-        gate(0, 1, g[0, 1], b_sb, 0, S)
-        quant_wa(0, 0, wa_bf)
-        with nc.allow_non_contiguous_dma(reason="one bias value a partition"):
-            nc.sync.dma_start(xop_col[:], xop.rearrange("(c p) -> p c", p=P))
+        cast_wa(0, wa_raw[0, 0])
+        gate(0, 1, b_sb, 0, S)
         g[1, 3] = load_g(1, 3)
         wc_raw = load_wc()
         b_sb = product_b(0, 2)
-        wa_bf = cast_wa(wa_raw[0, 1])
-        gate(0, 2, g[0, 2], b_sb, 0, S)
-        quant_wa(0, 1, wa_bf)
-        b_sb = product_b(0, 3)
-        a_sb = [product_a(0, lo, hi) for lo, hi in HALVES]
-        gate(0, 3, g[0, 3], b_sb, 0, S)
-        permute_wb(1)
-        h_bf = [add_h(0, a_sb[u], lo, hi) for u, (lo, hi) in enumerate(HALVES)]
-        b_next = product_b(1, 0)
-        for u, (lo, hi) in enumerate(HALVES):
-            quant_h(0, h_bf[u], lo, hi)
-
-        wa_bf = cast_wa(wa_raw[1, 0])
-        gate(1, 0, g[1, 0], b_next, 0, S)
-        quant_wa(1, 0, wa_bf)
+        cast_wa(1, wa_raw[0, 1])
+        b_next = product_b(0, 3)
+        gate(0, 2, b_sb, 0, S)
+        quant_wa(0)
+        b_sb = product_b(1, 0)
+        product_a(0)
+        gate(0, 3, b_next, 0, S)
+        gate(1, 0, b_sb, 0, S)
         b_sb = product_b(1, 1)
-        wa_bf = cast_wa(wa_raw[1, 1])
-        gate(1, 1, g[1, 1], b_sb, 0, S)
-        quant_wa(1, 1, wa_bf)
+        add_h(0, 0, S)
+        cast_wa(0, wa_raw[1, 0])
+        cast_wa(1, wa_raw[1, 1])
+        gate(1, 1, b_sb, 0, S)
+        quant_wa(1)
         b_sb = product_b(1, 2)
-        b_last = product_b(1, 3)
-        a_sb = [product_a(1, lo, hi) for lo, hi in HALVES]
-        gate(1, 2, g[1, 2], b_sb, 0, S)
-        wc_bf = keep.tile([P, 2, PACK * N], BF16, name="wc_bf", align_bytes=64)
+        b_next = product_b(1, 3)
+        product_a(1)
+        quant_h(0, 0, S)
+        gate(1, 2, b_sb, 0, S)
         for b in range(2):
             nc.scalar.copy(
                 wc_bf[:, b, :].rearrange("p (c i t) -> p c t i", i=2, t=PACK),
-                wc_raw[:, b].rearrange("p t (c i) -> p c t i", i=2),
+                wc_raw[:, b, :].rearrange("p (t c i) -> p c t i", i=2, t=PACK),
             )
-        for lo, hi in HALVES:
-            gate(1, 3, g[1, 3], b_last, lo, hi)
-        nc.vector.quantize_mx(
-            out=wcw[:].rearrange("p b n -> p (b n)").bitcast(FP8X4),
-            scales=wcs[:].rearrange("p b n -> p (b n)"),
-            in_=wc_bf[:].rearrange("p b n -> p (b n)"),
-        )
+        gate(1, 3, b_next, 0, S)
+        quant_wc()
         pending = None
         for lo, hi in TAIL:
-            tile = add_h(1, a_sb[lo // HALF], lo, hi)
+            add_h(1, lo, hi)
             if pending is not None:
                 quant_h(1, *pending)
-                decode(pending[1], pending[2], False)
-            pending = (tile, lo, hi)
+                decode(*pending, False)
+            pending = (lo, hi)
         quant_h(1, *pending)
-        decode(pending[1], pending[2], True)
+        decode(*pending, True)

@@ -19,10 +19,18 @@ ADD = mybir.AluOpType.add
 
 P = 128
 PACK = 4
-KP = P * PACK
-HALF = 512
-HALVES = [(0, 512), (512, 1024)]
-TAIL = [(0, 512), (512, 768), (768, 1024)]
+PASS = P * PACK
+PASSES = K // PASS
+BLOCKS = H // PASS
+OUT_TILES = N // P
+QUADS = 4
+GROUP = 16
+BANK = 512
+HALVES = [(lo, lo + BANK) for lo in range(0, S, BANK)]
+PIECE = 256
+PIECES = [(lo, lo + PIECE) for lo in range(0, S, PIECE)]
+STREAM_BUFS = 6
+B_BUFS = 4
 
 
 def tile_list_bilinear_koopman_step_kernel(
@@ -31,243 +39,229 @@ def tile_list_bilinear_koopman_step_kernel(
     nc = tc.nc
     with ExitStack() as ctx:
         keep = ctx.enter_context(tc.tile_pool(name="keep", bufs=1))
-        slab = ctx.enter_context(tc.tile_pool(name="slab", bufs=10))
-        bpool = ctx.enter_context(tc.tile_pool(name="bpool", bufs=4))
+        stream = ctx.enter_context(tc.tile_pool(name="stream", bufs=STREAM_BUFS))
+        b_pool = ctx.enter_context(tc.tile_pool(name="b_pool", bufs=B_BUFS))
         psum = ctx.enter_context(tc.psum_pool(name="psum", bufs=8))
 
-        offsets = keep.tile([P, S // 16], U16, name="offsets")
-        tsc = [keep.tile([P, 1, T], U8, name=f"tsc{a}", align_bytes=64) for a in range(2)]
-        wbs_raw = keep.tile([P, 2, H], U8, name="wbs_raw", align_bytes=64)
-        wbw_raw = keep.tile([P, 2, 2 * H], U8, name="wbw_raw", align_bytes=64)
-        wbw = keep.tile([P, PACK, 2, 2, 2 * P], U8, name="wbw", align_bytes=64)
-        wbs = keep.tile([P, PACK, 2, 2, P], U8, name="wbs", align_bytes=64)
-        vw = [keep.tile([P, S], U32, name=f"vw{a}", align_bytes=64) for a in range(2)]
-        vs = [keep.tile([P, S], U8, name=f"vs{a}", align_bytes=64) for a in range(2)]
-        waw = [keep.tile([P, 2, KP], U32, name=f"waw{b}", align_bytes=64) for b in range(2)]
-        was = [keep.tile([P, 2, KP], U8, name=f"was{b}", align_bytes=64) for b in range(2)]
-        wcw = keep.tile([P, 2, N], U32, name="wcw", align_bytes=64)
-        wcs = keep.tile([P, 2, N], U8, name="wcs", align_bytes=64)
-        wc_bf = keep.tile([P, 2, PACK * N], BF16, name="wc_bf", align_bytes=64)
-        hw = [keep.tile([P, S], U32, name=f"hw{b}", align_bytes=64) for b in range(2)]
-        hs = [keep.tile([P, S], U8, name=f"hs{b}", align_bytes=64) for b in range(2)]
-        h_bf = [keep.tile([P, PACK * S], BF16, name=f"h_bf{b}", align_bytes=64) for b in range(2)]
-        gb = [keep.tile([P, PACK, S], F32, name=f"gb{b}") for b in range(2)]
-        wa_bf = keep.tile([P, 2, PACK * KP], BF16, name="wa_bf", align_bytes=64)
-        a_sb = keep.tile([P, PACK, S], F32, name="a_sb")
-        res = keep.tile([P, 2 * S], F32, name="res")
-        drift_col = keep.tile([P, 2, PACK], F32, name="drift_col")
-        xop_col = keep.tile([P, 2], F32, name="xop_col")
+        def mx_tile(name, shape, dtype):
+            return keep.tile([P, *shape], dtype, name=name, tag=name, align_bytes=64)
+
+        offsets = keep.tile([P, S // GROUP], U16, name="offsets")
+        tab_sc = [mx_tile(f"tab_sc{a}", [1, T], U8) for a in range(PASSES)]
+        wb_sc_raw = mx_tile("wb_sc_raw", [PASSES, H], U8)
+        wb_wd_raw = mx_tile("wb_wd_raw", [PASSES, 2 * H], U8)
+        wb_wd = mx_tile("wb_wd", [PACK, PASSES, BLOCKS, 2 * P], U8)
+        wb_sc = mx_tile("wb_sc", [PACK, PASSES, BLOCKS, P], U8)
+        v_wd = [mx_tile(f"v_wd{a}", [S], U32) for a in range(PASSES)]
+        v_sc = [mx_tile(f"v_sc{a}", [S], U8) for a in range(PASSES)]
+        wa_wd = [mx_tile(f"wa_wd{b}", [PASSES, PASS], U32) for b in range(BLOCKS)]
+        wa_sc = [mx_tile(f"wa_sc{b}", [PASSES, PASS], U8) for b in range(BLOCKS)]
+        wa_bf = [mx_tile(f"wa_bf{b}", [PASSES, PACK * PASS], BF16) for b in range(BLOCKS)]
+        wc_wd = mx_tile("wc_wd", [BLOCKS, N], U32)
+        wc_sc = mx_tile("wc_sc", [BLOCKS, N], U8)
+        wc_bf = mx_tile("wc_bf", [BLOCKS, PACK * N], BF16)
+        h_wd = [mx_tile(f"h_wd{b}", [S], U32) for b in range(BLOCKS)]
+        h_sc = [mx_tile(f"h_sc{b}", [S], U8) for b in range(BLOCKS)]
+        h_bf = [mx_tile(f"h_bf{b}", [PACK * S], BF16) for b in range(BLOCKS)]
+        gated = [keep.tile([P, PACK, S], F32, name=f"gated{b}") for b in range(BLOCKS)]
+        auto_first = keep.tile([P, PACK, S], F32, name="auto_first")
+        auto_last = [keep.tile([P, PACK, BANK], F32, name=f"auto_last{u}") for u in range(len(HALVES))]
+        result = keep.tile([P, OUT_TILES * S], F32, name="result")
+        drift_col = keep.tile([P, BLOCKS, PACK], F32, name="drift_col")
+        xop_col = keep.tile([P, OUT_TILES], F32, name="xop_col", tag="wa_wd0", align_bytes=64)
 
         def load_table_words(a):
-            tile = slab.tile([P, T], I32, name="slab")
+            tile = stream.tile([P, T], I32, name="large")
             nc.sync.dma_start(tile[:], tab_words[a].rearrange("p t i -> p (t i)").bitcast(I32))
             return tile
 
         def load_g(b, t):
-            tile = slab.tile([P, T], F32, name="slab")
-            rows = gT[b * KP : (b + 1) * KP, :].rearrange("(p t) c -> p t c", t=PACK)
+            tile = stream.tile([P, T], F32, name="large")
+            rows = gT[b * PASS : (b + 1) * PASS, :].rearrange("(p t) c -> p t c", t=PACK)
             nc.sync.dma_start(tile[:], rows[:, t, :])
             return tile
 
         def load_wa(b, a):
-            tile = slab.tile([P, PACK, KP], F32, name="slab")
-            rows = wa[a * KP : (a + 1) * KP, b * KP : (b + 1) * KP]
-            nc.sync.dma_start(tile[:], rows.rearrange("(p j) c -> p j c", j=PACK))
+            tile = stream.tile([P, PACK, PASS], F32, name="large")
+            rows = wa[a * PASS : (a + 1) * PASS, b * PASS : (b + 1) * PASS]
+            nc.sync.dma_start(tile[:], rows.rearrange("(p i) c -> p i c", i=PACK))
             return tile
 
         def load_wc():
-            tile = slab.tile([P, 2, PACK * N], F32, name="slab")
-            nc.sync.dma_start(tile[:], wc.rearrange("(b p t) n -> p b (t n)", b=2, t=PACK))
+            tile = stream.tile([P, BLOCKS, PACK * N], F32, name="large")
+            nc.sync.dma_start(tile[:], wc.rearrange("(b p t) n -> p b (t n)", b=BLOCKS, t=PACK))
             return tile
 
-        def load_scales(tile, src):
-            for q in range(4):
-                rows = src[:, 4 * q : 4 * q + 4, :].rearrange("a r c -> r a c")
-                nc.sync.dma_start(tile[32 * q : 32 * q + 4, :, :].bitcast(I32), rows.bitcast(I32))
+        def load_scale_rows(tile, src):
+            for e in range(4):
+                rows = src[:, e :: 4, :].rearrange("a q c -> q a c")
+                nc.sync.dma_start(tile[e:P:32, :, :].bitcast(I32), rows.bitcast(I32))
 
         def listed(lo, hi):
-            return offsets[:, lo // 16 : hi // 16]
+            return offsets[:, lo // GROUP : hi // GROUP]
 
         def gather_scales(a, lo, hi):
-            nc.vector.tensor_copy(vs[a][:, lo:hi], tsc[a][:, 0, :].indirect(listed(lo, hi)))
+            nc.vector.tensor_copy(v_sc[a][:, lo:hi], tab_sc[a][:, 0, :].indirect(listed(lo, hi)))
 
-        def gather_words(a, window, lo, hi):
-            nc.vector.tensor_copy(vw[a][:, lo:hi], window[:].bitcast(U32).indirect(listed(lo, hi)))
+        def gather_words(a):
+            nc.vector.tensor_copy(v_wd[a][:], tab_wd[a][:].bitcast(U32).indirect(offsets[:]))
 
-        def permute_wb():
+        def reorder_wb():
             nc.vector.tensor_copy(
-                wbw[:].rearrange("p t a b c -> p t (a b c)").bitcast(U16),
-                wbw_raw[:].rearrange("p a c -> p (a c)").bitcast(U16).rearrange("p (x t) -> p t x", t=PACK),
+                wb_wd[:].rearrange("p t a b c -> p t (a b c)").bitcast(U16),
+                wb_wd_raw[:].rearrange("p a c -> p (a c)").bitcast(U16).rearrange("p (x t) -> p t x", t=PACK),
             )
             nc.vector.tensor_copy(
-                wbs[:].rearrange("p t a b c -> p t (a b c)"),
-                wbs_raw[:].rearrange("p a (x t) -> p t (a x)", t=PACK),
+                wb_sc[:].rearrange("p t a b c -> p t (a b c)"),
+                wb_sc_raw[:].rearrange("p a (x t) -> p t (a x)", t=PACK),
             )
 
-        def cast_wa(a, raw):
-            dst = wa_bf[:, a, :].rearrange("p (s i m j) -> p s m j i", s=2, i=2, j=PACK)
-            src = raw[:].rearrange("p j (m s i) -> p s m j i", s=2, i=2)
+        def quantize(words, scales, values):
+            nc.vector.quantize_mx(out=words.bitcast(FP8X4), scales=scales, in_=values)
+
+        def flat(tile):
+            return tile[:].rearrange("p a c -> p (a c)")
+
+        def round_wa(b, a):
+            dst = wa_bf[b][:, a, :].rearrange("p (s u m i) -> p s m i u", s=2, u=2, i=PACK)
+            src = wa_raw[b, a][:].rearrange("p i (m s u) -> p s m i u", s=2, u=2)
             for s in range(2):
                 nc.scalar.copy(dst[:, s], src[:, s])
 
-        def quant_wa(b):
-            nc.vector.quantize_mx(
-                out=waw[b][:].rearrange("p a c -> p (a c)").bitcast(FP8X4),
-                scales=was[b][:].rearrange("p a c -> p (a c)"),
-                in_=wa_bf[:].rearrange("p a c -> p (a c)"),
-            )
+        def interleaved(ap):
+            return ap.rearrange("p (c u t) -> p c t u", u=2, t=PACK)
 
-        def product_b(b, t):
-            b_sb = bpool.tile([P, S], F32, name="b_sb")
+        def by_pairs(ap):
+            return ap.rearrange("p t (c u) -> p c t u", u=2)
+
+        def mx_sum(width, operands):
+            acc = psum.tile([P, width], F32, name="acc")
+            for n, (lhs, lhs_sc, rhs, rhs_sc) in enumerate(operands):
+                nc.tensor.matmul_mx(
+                    out=acc[:],
+                    lhsT=lhs,
+                    lhsT_scale=lhs_sc,
+                    rhs=rhs.bitcast(FP8X4),
+                    rhs_scale=rhs_sc,
+                    start=(n == 0),
+                    stop=(n == len(operands) - 1),
+                )
+            return acc
+
+        def product_wb(b, t):
+            prod = b_pool.tile([P, S], F32, name="prod")
             for lo, hi in HALVES:
-                acc = psum.tile([P, HALF], F32, name="acc")
-                for a in range(2):
-                    nc.tensor.matmul_mx(
-                        out=acc[:],
-                        lhsT=wbw[:, t, a, b, :].bitcast(FP4X4),
-                        lhsT_scale=wbs[:, t, a, b, :],
-                        rhs=vw[a][:, lo:hi].bitcast(FP8X4),
-                        rhs_scale=vs[a][:, lo:hi],
-                        start=(a == 0),
-                        stop=(a == 1),
-                    )
-                nc.scalar.copy(b_sb[:, lo:hi], acc[:])
-            return b_sb
+                passes = [
+                    (wb_wd[:, t, a, b, :].bitcast(FP4X4), wb_sc[:, t, a, b, :], v_wd[a][:, lo:hi], v_sc[a][:, lo:hi])
+                    for a in range(PASSES)
+                ]
+                nc.scalar.copy(prod[:, lo:hi], mx_sum(BANK, passes)[:])
+            return prod
 
-        def product_a(b):
+        def auto_part(b, lo, hi):
+            if b == 0:
+                return auto_first[:, :, lo:hi]
+            return auto_last[lo // BANK][:, :, lo % BANK : lo % BANK + hi - lo]
+
+        def product_wa(b):
             for lo, hi in HALVES:
                 for t in range(PACK):
-                    acc = psum.tile([P, HALF], F32, name="acc")
-                    for a in range(2):
-                        nc.tensor.matmul_mx(
-                            out=acc[:],
-                            lhsT=waw[b][:, a, P * t : P * (t + 1)].bitcast(FP8X4),
-                            lhsT_scale=was[b][:, a, P * t : P * (t + 1)],
-                            rhs=vw[a][:, lo:hi].bitcast(FP8X4),
-                            rhs_scale=vs[a][:, lo:hi],
-                            start=(a == 0),
-                            stop=(a == 1),
-                        )
-                    nc.scalar.activation(a_sb[:, t, lo:hi], acc[:], IDENT, bias=drift_col[:, b, t : t + 1])
+                    cols = slice(P * t, P * (t + 1))
+                    passes = [
+                        (wa_wd[b][:, a, cols].bitcast(FP8X4), wa_sc[b][:, a, cols], v_wd[a][:, lo:hi], v_sc[a][:, lo:hi])
+                        for a in range(PASSES)
+                    ]
+                    acc = mx_sum(BANK, passes)
+                    nc.scalar.activation(auto_part(b, lo, hi)[:, t, :], acc[:], IDENT, bias=drift_col[:, b, t : t + 1])
 
-        def gate(b, t, b_sb, lo, hi):
-            nc.vector.tensor_tensor(gb[b][:, t, lo:hi], g[b, t][:].indirect(listed(lo, hi)), b_sb[:, lo:hi], MULT)
+        def gate(b, t, lo, hi):
+            window = g_raw[b, t][:].indirect(listed(lo, hi))
+            nc.vector.tensor_tensor(gated[b][:, t, lo:hi], window, wb_prod[b, t][:, lo:hi], MULT)
 
         def add_h(b, lo, hi):
-            nc.vector.tensor_tensor(
-                h_bf[b][:, PACK * lo : PACK * hi].rearrange("p (c i t) -> p c t i", i=2, t=PACK),
-                a_sb[:, :, lo:hi].rearrange("p t (c i) -> p c t i", i=2),
-                gb[b][:, :, lo:hi].rearrange("p t (c i) -> p c t i", i=2),
-                ADD,
-            )
+            dst = interleaved(h_bf[b][:, PACK * lo : PACK * hi])
+            nc.vector.tensor_tensor(dst, by_pairs(auto_part(b, lo, hi)), by_pairs(gated[b][:, :, lo:hi]), ADD)
 
-        def quant_h(b, lo, hi):
-            nc.vector.quantize_mx(
-                out=hw[b][:, lo:hi].bitcast(FP8X4), scales=hs[b][:, lo:hi], in_=h_bf[b][:, PACK * lo : PACK * hi]
-            )
+        def quantize_h(b, lo, hi):
+            quantize(h_wd[b][:, lo:hi], h_sc[b][:, lo:hi], h_bf[b][:, PACK * lo : PACK * hi])
 
-        def quant_wc():
-            nc.vector.quantize_mx(
-                out=wcw[:].rearrange("p b n -> p (b n)").bitcast(FP8X4),
-                scales=wcs[:].rearrange("p b n -> p (b n)"),
-                in_=wc_bf[:].rearrange("p b n -> p (b n)"),
-            )
-
-        def decode(lo, hi, share):
-            piece = res[:, 2 * lo : 2 * hi].rearrange("p (c j) -> p c j", c=2)
-            for c in range(2):
-                acc = psum.tile([P, hi - lo], F32, name="acc")
-                for b in range(2):
-                    nc.tensor.matmul_mx(
-                        out=acc[:],
-                        lhsT=wcw[:, b, P * c : P * (c + 1)].bitcast(FP8X4),
-                        lhsT_scale=wcs[:, b, P * c : P * (c + 1)],
-                        rhs=hw[b][:, lo:hi].bitcast(FP8X4),
-                        rhs_scale=hs[b][:, lo:hi],
-                        start=(b == 0),
-                        stop=(b == 1),
-                    )
-                if share and c == 1:
+        def decode(lo, hi):
+            piece = result[:, OUT_TILES * lo : OUT_TILES * hi].rearrange("p (c j) -> p c j", c=OUT_TILES)
+            for c in range(OUT_TILES):
+                cols = slice(P * c, P * (c + 1))
+                passes = [
+                    (wc_wd[:, b, cols].bitcast(FP8X4), wc_sc[:, b, cols], h_wd[b][:, lo:hi], h_sc[b][:, lo:hi])
+                    for b in range(BLOCKS)
+                ]
+                acc = mx_sum(hi - lo, passes)
+                if hi == S and c == OUT_TILES - 1:
                     nc.vector.tensor_scalar_add(piece[:, c, :], acc[:], xop_col[:, c : c + 1])
                 else:
                     nc.scalar.activation(piece[:, c, :], acc[:], IDENT, bias=xop_col[:, c : c + 1])
             nc.sync.dma_start(out[:, lo:hi].rearrange("(c p) j -> p c j", p=P), piece)
 
-        nc.vector.memset(tsc[1][:].bitcast(I32), 0)
-        nc.gpsimd.memset(wbs_raw[:].bitcast(I32), 0)
-        nc.sync.dma_start(offsets[:], offs)
-        for q in range(4):
-            rows = tab_scales[0, 4 * q : 4 * q + 4, :].bitcast(I32)
-            nc.sync.dma_start(tsc[0][32 * q : 32 * q + 32, 0, :].bitcast(I32), rows.unsqueeze(0).broadcast_to([8, 4, T // 4]))
-        tw = [load_table_words(a) for a in range(2)]
-        nc.sync.dma_start(wbw_raw[:].bitcast(I32), wb_words.rearrange("a p c -> p a c").bitcast(I32))
-        load_scales(tsc[1], tab_scales[1:2])
-        g = {}
-        wa_raw = {}
-        g[0, 0] = load_g(0, 0)
-        load_scales(wbs_raw, wb_scales)
-        wa_raw[0, 0] = load_wa(0, 0)
-        g[0, 1] = load_g(0, 1)
-        wa_raw[0, 1] = load_wa(0, 1)
-        nc.sync.dma_start(drift_col[:], drift.rearrange("(b p t) -> p b t", b=2, t=PACK))
-        g[0, 2] = load_g(0, 2)
-        g[0, 3] = load_g(0, 3)
-        g[1, 0] = load_g(1, 0)
-        with nc.allow_non_contiguous_dma(reason="one bias value a partition"):
-            nc.sync.dma_start(xop_col[:], xop.rearrange("(c p) -> p c", p=P))
-        wa_raw[1, 0] = load_wa(1, 0)
+        nc.vector.memset(tab_sc[1][:].bitcast(I32), 0)
+        nc.gpsimd.memset(wb_sc_raw[:].bitcast(I32), 0)
 
+        nc.sync.dma_start(offsets[:], offs)
+        for q in range(QUADS):
+            rows = tab_scales[0, 4 * q : 4 * q + 4, :].bitcast(I32).unsqueeze(0).broadcast_to([8, 4, T // 4])
+            nc.sync.dma_start(tab_sc[0][32 * q : 32 * q + 32, 0, :].bitcast(I32), rows)
+        tab_wd = [load_table_words(a) for a in range(PASSES)]
         gather_scales(0, 0, S)
-        gather_words(0, tw[0], 0, S)
-        gather_words(1, tw[1], 0, S)
-        permute_wb()
+
+        load_scale_rows(wb_sc_raw, wb_scales)
+        nc.sync.dma_start(wb_wd_raw[:].bitcast(I32), wb_words.rearrange("a p c -> p a c").bitcast(I32))
+        wa_raw = {(0, a): load_wa(0, a) for a in range(PASSES)}
+        load_scale_rows(tab_sc[1], tab_scales[1:2])
+        g_raw = {(0, 0): load_g(0, 0)}
+        for a in range(PASSES):
+            gather_words(a)
+        reorder_wb()
         for lo, hi in HALVES:
             gather_scales(1, lo, hi)
-        wa_raw[1, 1] = load_wa(1, 1)
-        g[1, 1] = load_g(1, 1)
 
-        b_sb = product_b(0, 0)
-        for lo, hi in HALVES:
-            gate(0, 0, b_sb, lo, hi)
-        g[1, 2] = load_g(1, 2)
-        b_sb = product_b(0, 1)
-        cast_wa(0, wa_raw[0, 0])
-        gate(0, 1, b_sb, 0, S)
-        g[1, 3] = load_g(1, 3)
+        g_raw[0, 1] = load_g(0, 1)
+        nc.sync.dma_start(drift_col[:], drift.rearrange("(b p t) -> p b t", b=BLOCKS, t=PACK))
+        for t in range(2, PACK):
+            g_raw[0, t] = load_g(0, t)
+        wa_raw[1, 0] = load_wa(1, 0)
+        g_raw[1, 0] = load_g(1, 0)
+        wa_raw[1, 1] = load_wa(1, 1)
+        for t in range(1, PACK):
+            g_raw[1, t] = load_g(1, t)
         wc_raw = load_wc()
-        b_sb = product_b(0, 2)
-        cast_wa(1, wa_raw[0, 1])
-        b_next = product_b(0, 3)
-        gate(0, 2, b_sb, 0, S)
-        quant_wa(0)
-        b_sb = product_b(1, 0)
-        product_a(0)
-        gate(0, 3, b_next, 0, S)
-        gate(1, 0, b_sb, 0, S)
-        b_sb = product_b(1, 1)
+
+        for a in range(PASSES):
+            round_wa(0, a)
+        quantize(flat(wa_wd[0]), flat(wa_sc[0]), flat(wa_bf[0]))
+        wb_prod = {(0, t): product_wb(0, t) for t in range(PACK)}
+        product_wa(0)
+        with nc.allow_non_contiguous_dma(reason="one bias value a partition"):
+            nc.sync.dma_start(xop_col[:], xop.rearrange("(c p) -> p c", p=P))
+        for lo, hi in HALVES:
+            gate(0, 0, lo, hi)
+        for t in range(1, PACK):
+            gate(0, t, 0, S)
         add_h(0, 0, S)
-        cast_wa(0, wa_raw[1, 0])
-        cast_wa(1, wa_raw[1, 1])
-        gate(1, 1, b_sb, 0, S)
-        quant_wa(1)
-        b_sb = product_b(1, 2)
-        b_next = product_b(1, 3)
-        product_a(1)
-        quant_h(0, 0, S)
-        gate(1, 2, b_sb, 0, S)
-        for b in range(2):
-            nc.scalar.copy(
-                wc_bf[:, b, :].rearrange("p (c i t) -> p c t i", i=2, t=PACK),
-                wc_raw[:, b, :].rearrange("p (t c i) -> p c t i", i=2, t=PACK),
-            )
-        gate(1, 3, b_next, 0, S)
-        quant_wc()
-        pending = None
-        for lo, hi in TAIL:
-            add_h(1, lo, hi)
-            if pending is not None:
-                quant_h(1, *pending)
-                decode(*pending, False)
-            pending = (lo, hi)
-        quant_h(1, *pending)
-        decode(*pending, True)
+
+        for a in range(PASSES):
+            round_wa(1, a)
+        quantize(flat(wa_wd[1]), flat(wa_sc[1]), flat(wa_bf[1]))
+        for t in range(PACK):
+            wb_prod[1, t] = product_wb(1, t)
+        gate(1, 0, 0, S)
+        quantize_h(0, 0, S)
+        for t in range(1, PACK):
+            gate(1, t, 0, S)
+        for b in range(BLOCKS):
+            nc.scalar.copy(interleaved(wc_bf[:, b, :]), by_pairs(wc_raw[:, b, :].rearrange("p (t n) -> p t n", t=PACK)))
+        product_wa(1)
+        quantize(flat(wc_wd), flat(wc_sc), flat(wc_bf))
+
+        add_h(1, *PIECES[0])
+        for n, (lo, hi) in enumerate(PIECES):
+            if n + 1 < len(PIECES):
+                add_h(1, *PIECES[n + 1])
+            quantize_h(1, lo, hi)
+            decode(lo, hi)

@@ -1,6 +1,7 @@
 from contextlib import ExitStack
 
 import concourse.mybir as mybir
+from concourse.masks import make_identity
 
 K, T, S, H, N = 1024, 2048, 1024, 1024, 256
 FLOPS = 2 * K * H * S * 2 + 2 * H * N * S
@@ -24,6 +25,7 @@ PASSES = K // PASS
 BLOCKS = H // PASS
 OUT_TILES = N // P
 QUADS = 4
+RUN = 8
 GROUP = 16
 BANK = 512
 HALVES = [(lo, lo + BANK) for lo in range(0, S, BANK)]
@@ -41,6 +43,8 @@ def tile_list_bilinear_koopman_step_kernel(
         keep = ctx.enter_context(tc.tile_pool(name="keep", bufs=1))
         stream = ctx.enter_context(tc.tile_pool(name="stream", bufs=STREAM_BUFS))
         b_pool = ctx.enter_context(tc.tile_pool(name="b_pool", bufs=B_BUFS))
+        h_pool = ctx.enter_context(tc.tile_pool(name="h_pool", bufs=1))
+        h_bf = {}
         psum = ctx.enter_context(tc.psum_pool(name="psum", bufs=8))
 
         def mx_tile(name, shape, dtype):
@@ -57,18 +61,16 @@ def tile_list_bilinear_koopman_step_kernel(
         wa_wd = [mx_tile(f"wa_wd{b}", [PASSES, PASS], U32) for b in range(BLOCKS)]
         wa_sc = [mx_tile(f"wa_sc{b}", [PASSES, PASS], U8) for b in range(BLOCKS)]
         wa_bf = [mx_tile(f"wa_bf{b}", [PASSES, PACK * PASS], BF16) for b in range(BLOCKS)]
-        wc_wd = mx_tile("wc_wd", [BLOCKS, N], U32)
         wc_sc = mx_tile("wc_sc", [BLOCKS, N], U8)
-        wc_bf = mx_tile("wc_bf", [BLOCKS, PACK * N], BF16)
-        h_wd = [mx_tile(f"h_wd{b}", [S], U32) for b in range(BLOCKS)]
+        h_wd = [mx_tile("h_wd0", [S], U32)]
         h_sc = [mx_tile(f"h_sc{b}", [S], U8) for b in range(BLOCKS)]
-        h_bf = [mx_tile(f"h_bf{b}", [PACK * S], BF16) for b in range(BLOCKS)]
         gated = [keep.tile([P, PACK, S], F32, name=f"gated{b}") for b in range(BLOCKS)]
         auto_first = keep.tile([P, PACK, S], F32, name="auto_first")
-        auto_last = [keep.tile([P, PACK, BANK], F32, name=f"auto_last{u}") for u in range(len(HALVES))]
+        auto_last = [mx_tile(f"auto_last{u}", [PACK, BANK], F32) for u in range(len(HALVES))]
         result = keep.tile([P, OUT_TILES * S], F32, name="result")
-        drift_col = keep.tile([P, BLOCKS, PACK], F32, name="drift_col")
-        xop_col = keep.tile([P, OUT_TILES], F32, name="xop_col", tag="wa_wd0", align_bytes=64)
+        bias_rows = keep.tile([P, P], F32, name="bias_rows")
+        identity = keep.tile([P, P], F32, name="identity")
+        bias = keep.tile([P, BLOCKS * PACK + OUT_TILES], F32, name="bias")
 
         def load_table_words(a):
             tile = stream.tile([P, T], I32, name="large")
@@ -77,8 +79,8 @@ def tile_list_bilinear_koopman_step_kernel(
 
         def load_g(b, t):
             tile = stream.tile([P, T], F32, name="large")
-            rows = gT[b * PASS : (b + 1) * PASS, :].rearrange("(p t) c -> p t c", t=PACK)
-            nc.sync.dma_start(tile[:], rows[:, t, :])
+            rows = gT[b * PASS : (b + 1) * PASS, :].rearrange("(q t e) c -> t q e c", t=PACK, e=RUN)
+            nc.sync.dma_start(tile[:], rows[t])
             return tile
 
         def load_wa(b, a):
@@ -88,8 +90,11 @@ def tile_list_bilinear_koopman_step_kernel(
             return tile
 
         def load_wc():
-            tile = stream.tile([P, BLOCKS, PACK * N], F32, name="large")
-            nc.sync.dma_start(tile[:], wc.rearrange("(b p t) n -> p b (t n)", b=BLOCKS, t=PACK))
+            tile = stream.tile([P, BLOCKS, PACK, N], F32, name="large")
+            rows = wc.rearrange("(b q t e) n -> b t q e n", b=BLOCKS, t=PACK, e=RUN)
+            for b in range(BLOCKS):
+                for t in range(PACK):
+                    nc.sync.dma_start(tile[:, b, t, :], rows[b, t])
             return tile
 
         def load_scale_rows(tile, src):
@@ -107,14 +112,12 @@ def tile_list_bilinear_koopman_step_kernel(
             nc.vector.tensor_copy(v_wd[a][:], tab_wd[a][:].bitcast(U32).indirect(offsets[:]))
 
         def reorder_wb():
-            nc.vector.tensor_copy(
-                wb_wd[:].rearrange("p t a b c -> p t (a b c)").bitcast(U16),
-                wb_wd_raw[:].rearrange("p a c -> p (a c)").bitcast(U16).rearrange("p (x t) -> p t x", t=PACK),
-            )
-            nc.vector.tensor_copy(
-                wb_sc[:].rearrange("p t a b c -> p t (a b c)"),
-                wb_sc_raw[:].rearrange("p a (x t) -> p t (a x)", t=PACK),
-            )
+            for dst, src in ((wb_wd, wb_wd_raw), (wb_sc, wb_sc_raw)):
+                runs = PASSES * H // (PACK * RUN)
+                nc.vector.tensor_copy(
+                    dst[:].rearrange("p t a b c -> p (t a b c)").bitcast(I32).rearrange("p (t x w) -> p t x w", t=PACK, x=runs),
+                    src[:].rearrange("p a c -> p (a c)").bitcast(I32).rearrange("p (x t w) -> p t x w", t=PACK, x=runs),
+                )
 
         def quantize(words, scales, values):
             nc.vector.quantize_mx(out=words.bitcast(FP8X4), scales=scales, in_=values)
@@ -122,11 +125,11 @@ def tile_list_bilinear_koopman_step_kernel(
         def flat(tile):
             return tile[:].rearrange("p a c -> p (a c)")
 
-        def round_wa(b, a):
-            dst = wa_bf[b][:, a, :].rearrange("p (s u m i) -> p s m i u", s=2, u=2, i=PACK)
-            src = wa_raw[b, a][:].rearrange("p i (m s u) -> p s m i u", s=2, u=2)
+        def round_wa(b, a, copy=nc.scalar.copy):
+            dst = wa_bf[b][:, a, :].rearrange("p (t q s u i) -> p s q t i u", t=PACK, s=2, u=4, i=PACK)
+            src = wa_raw[b, a][:].rearrange("p i (q t s u) -> p s q t i u", t=PACK, s=2, u=4)
             for s in range(2):
-                nc.scalar.copy(dst[:, s], src[:, s])
+                copy(dst[:, s], src[:, s])
 
         def interleaved(ap):
             return ap.rearrange("p (c u t) -> p c t u", u=2, t=PACK)
@@ -172,36 +175,45 @@ def tile_list_bilinear_koopman_step_kernel(
                         for a in range(PASSES)
                     ]
                     acc = mx_sum(BANK, passes)
-                    nc.scalar.activation(auto_part(b, lo, hi)[:, t, :], acc[:], IDENT, bias=drift_col[:, b, t : t + 1])
+                    nc.scalar.activation(auto_part(b, lo, hi)[:, t, :], acc[:], IDENT, bias=bias[:, PACK * b + t : PACK * b + t + 1])
 
         def gate(b, t, lo, hi):
             window = g_raw[b, t][:].indirect(listed(lo, hi))
             nc.vector.tensor_tensor(gated[b][:, t, lo:hi], window, wb_prod[b, t][:, lo:hi], MULT)
 
         def add_h(b, lo, hi):
-            dst = interleaved(h_bf[b][:, PACK * lo : PACK * hi])
+            name = f"h_bf{b}"
+            h_bf[b, lo] = h_pool.tile([P, PACK * (hi - lo)], BF16, name=name, tag=name, bufs=b + 1, align_bytes=64)
+            dst = interleaved(h_bf[b, lo][:])
             nc.vector.tensor_tensor(dst, by_pairs(auto_part(b, lo, hi)), by_pairs(gated[b][:, :, lo:hi]), ADD)
 
         def quantize_h(b, lo, hi):
-            quantize(h_wd[b][:, lo:hi], h_sc[b][:, lo:hi], h_bf[b][:, PACK * lo : PACK * hi])
+            quantize(h_wd[b][:, lo:hi], h_sc[b][:, lo:hi], h_bf[b, lo][:])
 
         def decode(lo, hi):
             piece = result[:, OUT_TILES * lo : OUT_TILES * hi].rearrange("p (c j) -> p c j", c=OUT_TILES)
             for c in range(OUT_TILES):
                 cols = slice(P * c, P * (c + 1))
+                xop_col = bias[:, BLOCKS * PACK + c : BLOCKS * PACK + c + 1]
                 passes = [
                     (wc_wd[:, b, cols].bitcast(FP8X4), wc_sc[:, b, cols], h_wd[b][:, lo:hi], h_sc[b][:, lo:hi])
                     for b in range(BLOCKS)
                 ]
                 acc = mx_sum(hi - lo, passes)
                 if hi == S and c == OUT_TILES - 1:
-                    nc.vector.tensor_scalar_add(piece[:, c, :], acc[:], xop_col[:, c : c + 1])
+                    nc.vector.tensor_scalar_add(piece[:, c, :], acc[:], xop_col)
                 else:
-                    nc.scalar.activation(piece[:, c, :], acc[:], IDENT, bias=xop_col[:, c : c + 1])
+                    nc.scalar.activation(piece[:, c, :], acc[:], IDENT, bias=xop_col)
             nc.sync.dma_start(out[:, lo:hi].rearrange("(c p) j -> p c j", p=P), piece)
 
         nc.vector.memset(tab_sc[1][:].bitcast(I32), 0)
         nc.gpsimd.memset(wb_sc_raw[:].bitcast(I32), 0)
+        nc.gpsimd.memset(bias_rows[:], 0.0)
+        for b in range(BLOCKS):
+            rows = drift.rearrange("(b q t e) -> b t q e", b=BLOCKS, t=PACK, e=RUN)[b]
+            nc.gpsimd.dma_start(bias_rows[PACK * b : PACK * (b + 1), :].rearrange("t (q e) -> t q e", e=RUN), rows)
+        nc.gpsimd.dma_start(bias_rows[BLOCKS * PACK : BLOCKS * PACK + OUT_TILES, :], xop.rearrange("(c p) -> c p", p=P))
+        make_identity(nc, identity[:])
 
         nc.sync.dma_start(offsets[:], offs)
         for q in range(QUADS):
@@ -210,19 +222,18 @@ def tile_list_bilinear_koopman_step_kernel(
         tab_wd = [load_table_words(a) for a in range(PASSES)]
         gather_scales(0, 0, S)
 
-        load_scale_rows(wb_sc_raw, wb_scales)
-        nc.sync.dma_start(wb_wd_raw[:].bitcast(I32), wb_words.rearrange("a p c -> p a c").bitcast(I32))
-        wa_raw = {(0, a): load_wa(0, a) for a in range(PASSES)}
         load_scale_rows(tab_sc[1], tab_scales[1:2])
+        nc.sync.dma_start(wb_wd_raw[:].bitcast(I32), wb_words.rearrange("a p c -> p a c").bitcast(I32))
+        wa_raw = {(0, 0): load_wa(0, 0)}
+        load_scale_rows(wb_sc_raw, wb_scales)
+        wa_raw[0, 1] = load_wa(0, 1)
         g_raw = {(0, 0): load_g(0, 0)}
         for a in range(PASSES):
             gather_words(a)
+        gather_scales(1, 0, S)
         reorder_wb()
-        for lo, hi in HALVES:
-            gather_scales(1, lo, hi)
 
         g_raw[0, 1] = load_g(0, 1)
-        nc.sync.dma_start(drift_col[:], drift.rearrange("(b p t) -> p b t", b=BLOCKS, t=PACK))
         for t in range(2, PACK):
             g_raw[0, t] = load_g(0, t)
         wa_raw[1, 0] = load_wa(1, 0)
@@ -232,13 +243,15 @@ def tile_list_bilinear_koopman_step_kernel(
             g_raw[1, t] = load_g(1, t)
         wc_raw = load_wc()
 
-        for a in range(PASSES):
-            round_wa(0, a)
-        quantize(flat(wa_wd[0]), flat(wa_sc[0]), flat(wa_bf[0]))
+        round_wa(0, 0)
+        quantize(wa_wd[0][:, 0, :], wa_sc[0][:, 0, :], wa_bf[0][:, 0, :])
+        round_wa(0, 1, copy=nc.vector.tensor_copy)
+        quantize(wa_wd[0][:, 1, :], wa_sc[0][:, 1, :], wa_bf[0][:, 1, :])
         wb_prod = {(0, t): product_wb(0, t) for t in range(PACK)}
+        turned = psum.tile([P, P], F32, name="acc")
+        nc.tensor.transpose(turned[:], bias_rows[:], identity[:])
+        nc.scalar.copy(bias[:], turned[:, 0 : BLOCKS * PACK + OUT_TILES])
         product_wa(0)
-        with nc.allow_non_contiguous_dma(reason="one bias value a partition"):
-            nc.sync.dma_start(xop_col[:], xop.rearrange("(c p) -> p c", p=P))
         for lo, hi in HALVES:
             gate(0, 0, lo, hi)
         for t in range(1, PACK):
@@ -254,14 +267,18 @@ def tile_list_bilinear_koopman_step_kernel(
         quantize_h(0, 0, S)
         for t in range(1, PACK):
             gate(1, t, 0, S)
-        for b in range(BLOCKS):
-            nc.scalar.copy(interleaved(wc_bf[:, b, :]), by_pairs(wc_raw[:, b, :].rearrange("p (t n) -> p t n", t=PACK)))
         product_wa(1)
-        quantize(flat(wc_wd), flat(wc_sc), flat(wc_bf))
+        wc_bf = keep.tile([P, BLOCKS, PACK * N], BF16, name="wc_bf", tag="wa_wd1", align_bytes=64)
+        for b in range(BLOCKS):
+            nc.scalar.copy(interleaved(wc_bf[:, b, :]), by_pairs(wc_raw[:, b]))
 
         add_h(1, *PIECES[0])
         for n, (lo, hi) in enumerate(PIECES):
             if n + 1 < len(PIECES):
                 add_h(1, *PIECES[n + 1])
+            if n == 0:
+                wc_wd = keep.tile([P, BLOCKS, N], U32, name="wc_wd", tag="auto_last0", align_bytes=64)
+                quantize(flat(wc_wd), flat(wc_sc), flat(wc_bf))
+                h_wd.append(keep.tile([P, S], U32, name="h_wd1", tag="wa_wd1", align_bytes=64))
             quantize_h(1, lo, hi)
             decode(lo, hi)

@@ -1,7 +1,6 @@
 from contextlib import ExitStack
 
 import concourse.mybir as mybir
-from concourse.masks import make_identity
 
 K, T, S, H, N = 1024, 2048, 1024, 1024, 256
 FLOPS = 2 * K * H * S * 2 + 2 * H * N * S
@@ -25,14 +24,12 @@ PASSES = K // PASS
 BLOCKS = H // PASS
 OUT_TILES = N // P
 QUADS = 4
-RUN = 8
 GROUP = 16
 BANK = 512
 HALVES = [(lo, lo + BANK) for lo in range(0, S, BANK)]
 PIECE = 256
-PIECES = [(lo, lo + PIECE) for lo in range(0, S, PIECE)]
+PIECES = [(lo, lo + PIECE) for lo in range(0, S - PIECE, PIECE)] + [(lo, lo + PIECE // 2) for lo in range(S - PIECE, S, PIECE // 2)]
 STREAM_BUFS = 6
-B_BUFS = 4
 
 
 def tile_list_bilinear_koopman_step_kernel(
@@ -42,7 +39,7 @@ def tile_list_bilinear_koopman_step_kernel(
     with ExitStack() as ctx:
         keep = ctx.enter_context(tc.tile_pool(name="keep", bufs=1))
         stream = ctx.enter_context(tc.tile_pool(name="stream", bufs=STREAM_BUFS))
-        b_pool = ctx.enter_context(tc.tile_pool(name="b_pool", bufs=B_BUFS))
+        b_pool = ctx.enter_context(tc.tile_pool(name="b_pool", bufs=1))
         h_pool = ctx.enter_context(tc.tile_pool(name="h_pool", bufs=1))
         h_bf = {}
         psum = ctx.enter_context(tc.psum_pool(name="psum", bufs=8))
@@ -68,9 +65,8 @@ def tile_list_bilinear_koopman_step_kernel(
         auto_first = keep.tile([P, PACK, S], F32, name="auto_first")
         auto_last = [mx_tile(f"auto_last{u}", [PACK, BANK], F32) for u in range(len(HALVES))]
         result = keep.tile([P, OUT_TILES * S], F32, name="result")
-        bias_rows = keep.tile([P, P], F32, name="bias_rows")
-        identity = keep.tile([P, P], F32, name="identity")
-        bias = keep.tile([P, BLOCKS * PACK + OUT_TILES], F32, name="bias")
+        drift_col = keep.tile([P, BLOCKS, PACK], F32, name="drift_col")
+        xop_col = keep.tile([P, OUT_TILES], F32, name="xop_col", tag="wa_wd0", align_bytes=64)
 
         def load_table_words(a):
             tile = stream.tile([P, T], I32, name="large")
@@ -79,22 +75,19 @@ def tile_list_bilinear_koopman_step_kernel(
 
         def load_g(b, t):
             tile = stream.tile([P, T], F32, name="large")
-            rows = gT[b * PASS : (b + 1) * PASS, :].rearrange("(q t e) c -> t q e c", t=PACK, e=RUN)
-            nc.sync.dma_start(tile[:], rows[t])
+            rows = gT[b * PASS : (b + 1) * PASS, :].rearrange("(p t) c -> p t c", t=PACK)
+            nc.sync.dma_start(tile[:], rows[:, t, :])
             return tile
 
-        def load_wa(b, a):
-            tile = stream.tile([P, PACK, PASS], F32, name="large")
+        def load_wa(b, a, pool=stream):
+            tile = pool.tile([P, PACK, PASS], F32, name="large" if pool is stream else "prod0")
             rows = wa[a * PASS : (a + 1) * PASS, b * PASS : (b + 1) * PASS]
             nc.sync.dma_start(tile[:], rows.rearrange("(p i) c -> p i c", i=PACK))
             return tile
 
         def load_wc():
-            tile = stream.tile([P, BLOCKS, PACK, N], F32, name="large")
-            rows = wc.rearrange("(b q t e) n -> b t q e n", b=BLOCKS, t=PACK, e=RUN)
-            for b in range(BLOCKS):
-                for t in range(PACK):
-                    nc.sync.dma_start(tile[:, b, t, :], rows[b, t])
+            tile = stream.tile([P, BLOCKS, PACK * N], F32, name="large")
+            nc.sync.dma_start(tile[:], wc.rearrange("(b p t) n -> p b (t n)", b=BLOCKS, t=PACK))
             return tile
 
         def load_scale_rows(tile, src):
@@ -112,12 +105,14 @@ def tile_list_bilinear_koopman_step_kernel(
             nc.vector.tensor_copy(v_wd[a][:], tab_wd[a][:].bitcast(U32).indirect(offsets[:]))
 
         def reorder_wb():
-            for dst, src in ((wb_wd, wb_wd_raw), (wb_sc, wb_sc_raw)):
-                runs = PASSES * H // (PACK * RUN)
-                nc.vector.tensor_copy(
-                    dst[:].rearrange("p t a b c -> p (t a b c)").bitcast(I32).rearrange("p (t x w) -> p t x w", t=PACK, x=runs),
-                    src[:].rearrange("p a c -> p (a c)").bitcast(I32).rearrange("p (x t w) -> p t x w", t=PACK, x=runs),
-                )
+            nc.vector.tensor_copy(
+                wb_wd[:].rearrange("p t a b c -> p t (a b c)").bitcast(U16),
+                wb_wd_raw[:].rearrange("p a c -> p (a c)").bitcast(U16).rearrange("p (x t) -> p t x", t=PACK),
+            )
+            nc.vector.tensor_copy(
+                wb_sc[:].rearrange("p t a b c -> p t (a b c)"),
+                wb_sc_raw[:].rearrange("p a (x t) -> p t (a x)", t=PACK),
+            )
 
         def quantize(words, scales, values):
             nc.vector.quantize_mx(out=words.bitcast(FP8X4), scales=scales, in_=values)
@@ -125,11 +120,11 @@ def tile_list_bilinear_koopman_step_kernel(
         def flat(tile):
             return tile[:].rearrange("p a c -> p (a c)")
 
-        def round_wa(b, a, copy=nc.scalar.copy):
-            dst = wa_bf[b][:, a, :].rearrange("p (t q s u i) -> p s q t i u", t=PACK, s=2, u=4, i=PACK)
-            src = wa_raw[b, a][:].rearrange("p i (q t s u) -> p s q t i u", t=PACK, s=2, u=4)
-            for s in range(2):
-                copy(dst[:, s], src[:, s])
+        def round_wa(b, a, second=nc.scalar.copy):
+            dst = wa_bf[b][:, a, :].rearrange("p (s u m i) -> p s m i u", s=2, u=2, i=PACK)
+            src = wa_raw[b, a][:].rearrange("p i (m s u) -> p s m i u", s=2, u=2)
+            nc.scalar.copy(dst[:, 0], src[:, 0])
+            second(dst[:, 1], src[:, 1])
 
         def interleaved(ap):
             return ap.rearrange("p (c u t) -> p c t u", u=2, t=PACK)
@@ -137,28 +132,32 @@ def tile_list_bilinear_koopman_step_kernel(
         def by_pairs(ap):
             return ap.rearrange("p t (c u) -> p c t u", u=2)
 
+        def mx_pass(acc, n, count, lhs, lhs_sc, rhs, rhs_sc):
+            nc.tensor.matmul_mx(
+                out=acc[:],
+                lhsT=lhs,
+                lhsT_scale=lhs_sc,
+                rhs=rhs.bitcast(FP8X4),
+                rhs_scale=rhs_sc,
+                start=(n == 0),
+                stop=(n == count - 1),
+            )
+
         def mx_sum(width, operands):
             acc = psum.tile([P, width], F32, name="acc")
-            for n, (lhs, lhs_sc, rhs, rhs_sc) in enumerate(operands):
-                nc.tensor.matmul_mx(
-                    out=acc[:],
-                    lhsT=lhs,
-                    lhsT_scale=lhs_sc,
-                    rhs=rhs.bitcast(FP8X4),
-                    rhs_scale=rhs_sc,
-                    start=(n == 0),
-                    stop=(n == len(operands) - 1),
-                )
+            for n, operand in enumerate(operands):
+                mx_pass(acc, n, len(operands), *operand)
             return acc
 
-        def product_wb(b, t):
-            prod = b_pool.tile([P, S], F32, name="prod")
-            for lo, hi in HALVES:
-                passes = [
-                    (wb_wd[:, t, a, b, :].bitcast(FP4X4), wb_sc[:, t, a, b, :], v_wd[a][:, lo:hi], v_sc[a][:, lo:hi])
-                    for a in range(PASSES)
-                ]
-                nc.scalar.copy(prod[:, lo:hi], mx_sum(BANK, passes)[:])
+        def product_wb(b):
+            prod = b_pool.tile([P, PACK, S], F32, name=f"prod{b}")
+            for t in range(PACK):
+                for lo, hi in HALVES:
+                    passes = [
+                        (wb_wd[:, t, a, b, :].bitcast(FP4X4), wb_sc[:, t, a, b, :], v_wd[a][:, lo:hi], v_sc[a][:, lo:hi])
+                        for a in range(PASSES)
+                    ]
+                    nc.scalar.copy(prod[:, t, lo:hi], mx_sum(BANK, passes)[:])
             return prod
 
         def auto_part(b, lo, hi):
@@ -175,11 +174,11 @@ def tile_list_bilinear_koopman_step_kernel(
                         for a in range(PASSES)
                     ]
                     acc = mx_sum(BANK, passes)
-                    nc.scalar.activation(auto_part(b, lo, hi)[:, t, :], acc[:], IDENT, bias=bias[:, PACK * b + t : PACK * b + t + 1])
+                    nc.scalar.activation(auto_part(b, lo, hi)[:, t, :], acc[:], IDENT, bias=drift_col[:, b, t : t + 1])
 
         def gate(b, t, lo, hi):
             window = g_raw[b, t][:].indirect(listed(lo, hi))
-            nc.vector.tensor_tensor(gated[b][:, t, lo:hi], window, wb_prod[b, t][:, lo:hi], MULT)
+            nc.vector.tensor_tensor(gated[b][:, t, lo:hi], window, wb_prod[b][:, t, lo:hi], MULT)
 
         def add_h(b, lo, hi):
             name = f"h_bf{b}"
@@ -192,28 +191,23 @@ def tile_list_bilinear_koopman_step_kernel(
 
         def decode(lo, hi):
             piece = result[:, OUT_TILES * lo : OUT_TILES * hi].rearrange("p (c j) -> p c j", c=OUT_TILES)
-            for c in range(OUT_TILES):
-                cols = slice(P * c, P * (c + 1))
-                xop_col = bias[:, BLOCKS * PACK + c : BLOCKS * PACK + c + 1]
-                passes = [
-                    (wc_wd[:, b, cols].bitcast(FP8X4), wc_sc[:, b, cols], h_wd[b][:, lo:hi], h_sc[b][:, lo:hi])
-                    for b in range(BLOCKS)
-                ]
-                acc = mx_sum(hi - lo, passes)
-                if hi == S and c == OUT_TILES - 1:
-                    nc.vector.tensor_scalar_add(piece[:, c, :], acc[:], xop_col)
-                else:
-                    nc.scalar.activation(piece[:, c, :], acc[:], IDENT, bias=xop_col)
-            nc.sync.dma_start(out[:, lo:hi].rearrange("(c p) j -> p c j", p=P), piece)
+            accs = [psum.tile([P, hi - lo], F32, name="acc") for c in range(OUT_TILES)]
+            for b in range(BLOCKS):
+                for c in range(OUT_TILES):
+                    cols = slice(P * c, P * (c + 1))
+                    mx_pass(accs[c], b, BLOCKS, wc_wd[:, b, cols].bitcast(FP8X4), wc_sc[:, b, cols], h_wd[b][:, lo:hi], h_sc[b][:, lo:hi])
+            rows = out[:, lo:hi].rearrange("(c p) j -> p c j", p=P)
+            nc.scalar.activation(piece[:, 0, :], accs[0][:], IDENT, bias=xop_col[:, 0:1])
+            if hi < S:
+                nc.scalar.activation(piece[:, 1, :], accs[1][:], IDENT, bias=xop_col[:, 1:2])
+                nc.sync.dma_start(rows, piece)
+            else:
+                nc.vector.tensor_scalar_add(piece[:, 1, :], accs[1][:], xop_col[:, 1:2])
+                nc.scalar.dma_start(rows[:, 0, :], piece[:, 0, :])
+                nc.sync.dma_start(rows[:, 1, :], piece[:, 1, :])
 
         nc.vector.memset(tab_sc[1][:].bitcast(I32), 0)
         nc.gpsimd.memset(wb_sc_raw[:].bitcast(I32), 0)
-        nc.gpsimd.memset(bias_rows[:], 0.0)
-        for b in range(BLOCKS):
-            rows = drift.rearrange("(b q t e) -> b t q e", b=BLOCKS, t=PACK, e=RUN)[b]
-            nc.gpsimd.dma_start(bias_rows[PACK * b : PACK * (b + 1), :].rearrange("t (q e) -> t q e", e=RUN), rows)
-        nc.gpsimd.dma_start(bias_rows[BLOCKS * PACK : BLOCKS * PACK + OUT_TILES, :], xop.rearrange("(c p) -> c p", p=P))
-        make_identity(nc, identity[:])
 
         nc.sync.dma_start(offsets[:], offs)
         for q in range(QUADS):
@@ -226,7 +220,7 @@ def tile_list_bilinear_koopman_step_kernel(
         nc.sync.dma_start(wb_wd_raw[:].bitcast(I32), wb_words.rearrange("a p c -> p a c").bitcast(I32))
         wa_raw = {(0, 0): load_wa(0, 0)}
         load_scale_rows(wb_sc_raw, wb_scales)
-        wa_raw[0, 1] = load_wa(0, 1)
+        wa_raw[0, 1] = load_wa(0, 1, pool=b_pool)
         g_raw = {(0, 0): load_g(0, 0)}
         for a in range(PASSES):
             gather_words(a)
@@ -234,6 +228,7 @@ def tile_list_bilinear_koopman_step_kernel(
         reorder_wb()
 
         g_raw[0, 1] = load_g(0, 1)
+        nc.sync.dma_start(drift_col[:], drift.rearrange("(b p t) -> p b t", b=BLOCKS, t=PACK))
         for t in range(2, PACK):
             g_raw[0, t] = load_g(0, t)
         wa_raw[1, 0] = load_wa(1, 0)
@@ -245,13 +240,12 @@ def tile_list_bilinear_koopman_step_kernel(
 
         round_wa(0, 0)
         quantize(wa_wd[0][:, 0, :], wa_sc[0][:, 0, :], wa_bf[0][:, 0, :])
-        round_wa(0, 1, copy=nc.vector.tensor_copy)
+        round_wa(0, 1, second=nc.vector.tensor_copy)
         quantize(wa_wd[0][:, 1, :], wa_sc[0][:, 1, :], wa_bf[0][:, 1, :])
-        wb_prod = {(0, t): product_wb(0, t) for t in range(PACK)}
-        turned = psum.tile([P, P], F32, name="acc")
-        nc.tensor.transpose(turned[:], bias_rows[:], identity[:])
-        nc.scalar.copy(bias[:], turned[:, 0 : BLOCKS * PACK + OUT_TILES])
+        wb_prod = [product_wb(0)]
         product_wa(0)
+        with nc.allow_non_contiguous_dma(reason="one bias value a partition"):
+            nc.sync.dma_start(xop_col[:], xop.rearrange("(c p) -> p c", p=P))
         for lo, hi in HALVES:
             gate(0, 0, lo, hi)
         for t in range(1, PACK):
@@ -261,8 +255,7 @@ def tile_list_bilinear_koopman_step_kernel(
         for a in range(PASSES):
             round_wa(1, a)
         quantize(flat(wa_wd[1]), flat(wa_sc[1]), flat(wa_bf[1]))
-        for t in range(PACK):
-            wb_prod[1, t] = product_wb(1, t)
+        wb_prod.append(product_wb(1))
         gate(1, 0, 0, S)
         quantize_h(0, 0, S)
         for t in range(1, PACK):
@@ -270,7 +263,7 @@ def tile_list_bilinear_koopman_step_kernel(
         product_wa(1)
         wc_bf = keep.tile([P, BLOCKS, PACK * N], BF16, name="wc_bf", tag="wa_wd1", align_bytes=64)
         for b in range(BLOCKS):
-            nc.scalar.copy(interleaved(wc_bf[:, b, :]), by_pairs(wc_raw[:, b]))
+            nc.scalar.copy(interleaved(wc_bf[:, b, :]), by_pairs(wc_raw[:, b, :].rearrange("p (t n) -> p t n", t=PACK)))
 
         add_h(1, *PIECES[0])
         for n, (lo, hi) in enumerate(PIECES):

@@ -29,7 +29,8 @@ BANK = 512
 HALVES = [(lo, lo + BANK) for lo in range(0, S, BANK)]
 PIECE = 256
 PIECES = [(lo, lo + PIECE) for lo in range(0, S - PIECE, PIECE)] + [(lo, lo + PIECE // 2) for lo in range(S - PIECE, S, PIECE // 2)]
-STREAM_BUFS = 6
+STREAM_BUFS = 5
+BUF_BYTES = 4 * T
 
 
 def tile_list_bilinear_koopman_step_kernel(
@@ -38,7 +39,7 @@ def tile_list_bilinear_koopman_step_kernel(
     nc = tc.nc
     with ExitStack() as ctx:
         keep = ctx.enter_context(tc.tile_pool(name="keep", bufs=1))
-        stream = ctx.enter_context(tc.tile_pool(name="stream", bufs=STREAM_BUFS))
+        stream = ctx.enter_context(tc.tile_pool(name="stream", bufs=1))
         b_pool = ctx.enter_context(tc.tile_pool(name="b_pool", bufs=1))
         h_pool = ctx.enter_context(tc.tile_pool(name="h_pool", bufs=1))
         h_bf = {}
@@ -48,16 +49,23 @@ def tile_list_bilinear_koopman_step_kernel(
             return keep.tile([P, *shape], dtype, name=name, tag=name, align_bytes=64)
 
         offsets = keep.tile([P, S // GROUP], U16, name="offsets")
-        tab_sc = [mx_tile(f"tab_sc{a}", [1, T], U8) for a in range(PASSES)]
+
+        def large(buf, shape, dtype):
+            name = f"large{buf}"
+            return stream.tile([P, *shape], dtype, name=name, tag=name, align_bytes=64, offset=buf * BUF_BYTES)
+
+        tab_wd = [large(a, [T], I32) for a in range(PASSES)]
+        end = STREAM_BUFS * BUF_BYTES
+        tab_sc = stream.tile([P, T], U8, name="tab_sc", align_bytes=64, offset=end - T // 2)
+        v_wd = [mx_tile("v_wd0", [S], U32), stream.tile([P, S], U32, name="v_wd1", align_bytes=64, offset=end)]
         wb_sc_raw = mx_tile("wb_sc_raw", [PASSES, H], U8)
         wb_wd_raw = mx_tile("wb_wd_raw", [PASSES, 2 * H], U8)
-        wb_wd = mx_tile("wb_wd", [PACK, PASSES, BLOCKS, 2 * P], U8)
-        wb_sc = mx_tile("wb_sc", [PACK, PASSES, BLOCKS, P], U8)
-        v_wd = [mx_tile(f"v_wd{a}", [S], U32) for a in range(PASSES)]
+        wb_wd = [mx_tile(f"wb_wd{b}", [PACK, PASSES, 2 * P], U8) for b in range(BLOCKS)]
+        wb_sc = [mx_tile(f"wb_sc{b}", [PACK, PASSES, P], U8) for b in range(BLOCKS)]
         v_sc = [mx_tile(f"v_sc{a}", [S], U8) for a in range(PASSES)]
         wa_wd = [mx_tile(f"wa_wd{b}", [PASSES, PASS], U32) for b in range(BLOCKS)]
         wa_sc = [mx_tile(f"wa_sc{b}", [PASSES, PASS], U8) for b in range(BLOCKS)]
-        wa_bf = [mx_tile(f"wa_bf{b}", [PASSES, PACK * PASS], BF16) for b in range(BLOCKS)]
+        wa_bf = [large(3, [PASSES, PACK * PASS], BF16), mx_tile("wa_bf1", [PASSES, PACK * PASS], BF16)]
         wc_sc = mx_tile("wc_sc", [BLOCKS, N], U8)
         h_wd = [mx_tile("h_wd0", [S], U32)]
         h_sc = [mx_tile(f"h_sc{b}", [S], U8) for b in range(BLOCKS)]
@@ -69,24 +77,22 @@ def tile_list_bilinear_koopman_step_kernel(
         xop_col = keep.tile([P, OUT_TILES], F32, name="xop_col", tag="wa_wd0", align_bytes=64)
 
         def load_table_words(a):
-            tile = stream.tile([P, T], I32, name="large")
-            nc.sync.dma_start(tile[:], tab_words[a].rearrange("p t i -> p (t i)").bitcast(I32))
-            return tile
+            nc.sync.dma_start(tab_wd[a][:], tab_words[a].rearrange("p t i -> p (t i)").bitcast(I32))
 
-        def load_g(b, t):
-            tile = stream.tile([P, T], F32, name="large")
+        def load_g(b, t, buf):
+            tile = large(buf, [T], F32)
             rows = gT[b * PASS : (b + 1) * PASS, :].rearrange("(p t) c -> p t c", t=PACK)
             nc.sync.dma_start(tile[:], rows[:, t, :])
             return tile
 
-        def load_wa(b, a, pool=stream):
-            tile = pool.tile([P, PACK, PASS], F32, name="large" if pool is stream else "prod0")
+        def load_wa(b, a, buf):
+            tile = large(buf, [PACK, PASS], F32)
             rows = wa[a * PASS : (a + 1) * PASS, b * PASS : (b + 1) * PASS]
             nc.sync.dma_start(tile[:], rows.rearrange("(p i) c -> p i c", i=PACK))
             return tile
 
-        def load_wc():
-            tile = stream.tile([P, BLOCKS, PACK * N], F32, name="large")
+        def load_wc(buf):
+            tile = large(buf, [BLOCKS, PACK * N], F32)
             nc.sync.dma_start(tile[:], wc.rearrange("(b p t) n -> p b (t n)", b=BLOCKS, t=PACK))
             return tile
 
@@ -98,21 +104,14 @@ def tile_list_bilinear_koopman_step_kernel(
         def listed(lo, hi):
             return offsets[:, lo // GROUP : hi // GROUP]
 
-        def gather_scales(a, lo, hi):
-            nc.vector.tensor_copy(v_sc[a][:, lo:hi], tab_sc[a][:, 0, :].indirect(listed(lo, hi)))
-
         def gather_words(a):
             nc.vector.tensor_copy(v_wd[a][:], tab_wd[a][:].bitcast(U32).indirect(offsets[:]))
 
-        def reorder_wb():
-            nc.vector.tensor_copy(
-                wb_wd[:].rearrange("p t a b c -> p t (a b c)").bitcast(U16),
-                wb_wd_raw[:].rearrange("p a c -> p (a c)").bitcast(U16).rearrange("p (x t) -> p t x", t=PACK),
-            )
-            nc.vector.tensor_copy(
-                wb_sc[:].rearrange("p t a b c -> p t (a b c)"),
-                wb_sc_raw[:].rearrange("p a (x t) -> p t (a x)", t=PACK),
-            )
+        def reorder_wb(b):
+            words = wb_wd_raw[:].bitcast(U16)[:, :, b * PASS : (b + 1) * PASS]
+            scales = wb_sc_raw[:, :, b * PASS : (b + 1) * PASS]
+            nc.vector.tensor_copy(wb_wd[b][:].bitcast(U16), words.rearrange("p a (m t) -> p t a m", t=PACK))
+            nc.vector.tensor_copy(wb_sc[b][:], scales.rearrange("p a (m t) -> p t a m", t=PACK))
 
         def quantize(words, scales, values):
             nc.vector.quantize_mx(out=words.bitcast(FP8X4), scales=scales, in_=values)
@@ -120,11 +119,11 @@ def tile_list_bilinear_koopman_step_kernel(
         def flat(tile):
             return tile[:].rearrange("p a c -> p (a c)")
 
-        def round_wa(b, a, second=nc.scalar.copy):
+        def round_wa(b, a):
             dst = wa_bf[b][:, a, :].rearrange("p (s u m i) -> p s m i u", s=2, u=2, i=PACK)
             src = wa_raw[b, a][:].rearrange("p i (m s u) -> p s m i u", s=2, u=2)
-            nc.scalar.copy(dst[:, 0], src[:, 0])
-            second(dst[:, 1], src[:, 1])
+            for s in range(2):
+                nc.scalar.copy(dst[:, s], src[:, s])
 
         def interleaved(ap):
             return ap.rearrange("p (c u t) -> p c t u", u=2, t=PACK)
@@ -154,8 +153,8 @@ def tile_list_bilinear_koopman_step_kernel(
             for t in range(PACK):
                 for lo, hi in HALVES:
                     passes = [
-                        (wb_wd[:, t, a, b, :].bitcast(FP4X4), wb_sc[:, t, a, b, :], v_wd[a][:, lo:hi], v_sc[a][:, lo:hi])
-                        for a in range(PASSES)
+                        (wb_wd[b][:, t, a, :].bitcast(FP4X4), wb_sc[b][:, t, a, :], v_wd[a][:, lo:hi], v_sc[a][:, lo:hi])
+                        for a in reversed(range(PASSES))
                     ]
                     nc.scalar.copy(prod[:, t, lo:hi], mx_sum(BANK, passes)[:])
             return prod
@@ -206,42 +205,44 @@ def tile_list_bilinear_koopman_step_kernel(
                 nc.scalar.dma_start(rows[:, 0, :], piece[:, 0, :])
                 nc.sync.dma_start(rows[:, 1, :], piece[:, 1, :])
 
-        nc.vector.memset(tab_sc[1][:].bitcast(I32), 0)
-        nc.gpsimd.memset(wb_sc_raw[:].bitcast(I32), 0)
+        nc.gpsimd.memset(tab_sc[:].bitcast(I32), 0)
+        nc.vector.memset(wb_sc_raw[:].bitcast(I32), 0)
+        nc.vector.memset(v_sc[1][:].bitcast(I32), 0)
 
         nc.sync.dma_start(offsets[:], offs)
-        for q in range(QUADS):
-            rows = tab_scales[0, 4 * q : 4 * q + 4, :].bitcast(I32).unsqueeze(0).broadcast_to([8, 4, T // 4])
-            nc.sync.dma_start(tab_sc[0][32 * q : 32 * q + 32, 0, :].bitcast(I32), rows)
-        tab_wd = [load_table_words(a) for a in range(PASSES)]
-        gather_scales(0, 0, S)
-
-        load_scale_rows(tab_sc[1], tab_scales[1:2])
-        nc.sync.dma_start(wb_wd_raw[:].bitcast(I32), wb_words.rearrange("a p c -> p a c").bitcast(I32))
-        wa_raw = {(0, 0): load_wa(0, 0)}
-        load_scale_rows(wb_sc_raw, wb_scales)
-        wa_raw[0, 1] = load_wa(0, 1, pool=b_pool)
-        g_raw = {(0, 0): load_g(0, 0)}
         for a in range(PASSES):
-            gather_words(a)
-        gather_scales(1, 0, S)
-        reorder_wb()
+            load_table_words(a)
+        for e in range(4):
+            rows = tab_scales[:, e :: 4, :].rearrange("a q c -> q a c")
+            nc.sync.dma_start(tab_sc[e:P:16, :].bitcast(I32), rows.bitcast(I32))
+        nc.sync.dma_start(wb_wd_raw[:].bitcast(I32), wb_words.rearrange("a p c -> p a c").bitcast(I32))
+        wa_raw = {(0, 0): load_wa(0, 0, 2)}
+        load_scale_rows(wb_sc_raw, wb_scales)
+        wa_raw[0, 1] = load_wa(0, 1, 0)
+        gather_words(0)
+        nc.vector.tensor_copy(v_sc[0][:], tab_sc[:].indirect(offsets[:]))
+        nc.sync.dma_start(v_sc[1][0 : P - 16, :].bitcast(I32), v_sc[0][16:P, :].bitcast(I32))
+        gather_words(1)
+        g_raw = {(0, 0): load_g(0, 0, 4)}
+        for b in range(BLOCKS):
+            reorder_wb(b)
 
-        g_raw[0, 1] = load_g(0, 1)
+        g_raw[0, 1] = load_g(0, 1, 1)
         nc.sync.dma_start(drift_col[:], drift.rearrange("(b p t) -> p b t", b=BLOCKS, t=PACK))
-        for t in range(2, PACK):
-            g_raw[0, t] = load_g(0, t)
-        wa_raw[1, 0] = load_wa(1, 0)
-        g_raw[1, 0] = load_g(1, 0)
-        wa_raw[1, 1] = load_wa(1, 1)
-        for t in range(1, PACK):
-            g_raw[1, t] = load_g(1, t)
-        wc_raw = load_wc()
+        g_raw[0, 2] = load_g(0, 2, 2)
+        g_raw[0, 3] = load_g(0, 3, 0)
 
         round_wa(0, 0)
         quantize(wa_wd[0][:, 0, :], wa_sc[0][:, 0, :], wa_bf[0][:, 0, :])
-        round_wa(0, 1, second=nc.vector.tensor_copy)
+        round_wa(0, 1)
         quantize(wa_wd[0][:, 1, :], wa_sc[0][:, 1, :], wa_bf[0][:, 1, :])
+        wa_raw[1, 0] = load_wa(1, 0, 3)
+        g_raw[1, 0] = load_g(1, 0, 4)
+        wa_raw[1, 1] = load_wa(1, 1, 1)
+        g_raw[1, 1] = load_g(1, 1, 2)
+        g_raw[1, 2] = load_g(1, 2, 0)
+        g_raw[1, 3] = load_g(1, 3, 3)
+        wc_raw = load_wc(4)
         wb_prod = [product_wb(0)]
         product_wa(0)
         with nc.allow_non_contiguous_dma(reason="one bias value a partition"):

@@ -59,9 +59,9 @@ def tile_list_bilinear_koopman_step_kernel(
         tab_sc = stream.tile([P, T], U8, name="tab_sc", align_bytes=64, offset=end - T // 2)
         v_wd = [mx_tile("v_wd0", [S], U32), stream.tile([P, S], U32, name="v_wd1", align_bytes=64, offset=end)]
         wb_sc_raw = mx_tile("wb_sc_raw", [PASSES, H], U8)
-        wb_wd_raw = mx_tile("wb_wd_raw", [PASSES, 2 * H], U8)
+        wb_wd_raw = [mx_tile(f"wb_wd_raw{b}", [PASSES, 2 * PASS], U8) for b in range(BLOCKS)]
         wb_wd = [mx_tile(f"wb_wd{b}", [PACK, PASSES, 2 * P], U8) for b in range(BLOCKS)]
-        wb_sc = [mx_tile(f"wb_sc{b}", [PACK, PASSES, P], U8) for b in range(BLOCKS)]
+        wb_sc = [mx_tile("wb_sc0", [PACK, PASSES, P], U8)]
         v_sc = [mx_tile(f"v_sc{a}", [S], U8) for a in range(PASSES)]
         wa_wd = [mx_tile(f"wa_wd{b}", [PASSES, PASS], U32) for b in range(BLOCKS)]
         wa_sc = [mx_tile(f"wa_sc{b}", [PASSES, PASS], U8) for b in range(BLOCKS)]
@@ -108,7 +108,7 @@ def tile_list_bilinear_koopman_step_kernel(
             nc.vector.tensor_copy(v_wd[a][:], tab_wd[a][:].bitcast(U32).indirect(offsets[:]))
 
         def reorder_wb(b):
-            words = wb_wd_raw[:].bitcast(U16)[:, :, b * PASS : (b + 1) * PASS]
+            words = wb_wd_raw[b][:].bitcast(U16)
             scales = wb_sc_raw[:, :, b * PASS : (b + 1) * PASS]
             nc.vector.tensor_copy(wb_wd[b][:].bitcast(U16), words.rearrange("p a (m t) -> p t a m", t=PACK))
             nc.vector.tensor_copy(wb_sc[b][:], scales.rearrange("p a (m t) -> p t a m", t=PACK))
@@ -181,7 +181,7 @@ def tile_list_bilinear_koopman_step_kernel(
 
         def add_h(b, lo, hi):
             name = f"h_bf{b}"
-            h_bf[b, lo] = h_pool.tile([P, PACK * (hi - lo)], BF16, name=name, tag=name, bufs=b + 1, align_bytes=64)
+            h_bf[b, lo] = h_pool.tile([P, PACK * (hi - lo)], BF16, name=name, tag=name, bufs=2, align_bytes=64)
             dst = interleaved(h_bf[b, lo][:])
             nc.vector.tensor_tensor(dst, by_pairs(auto_part(b, lo, hi)), by_pairs(gated[b][:, :, lo:hi]), ADD)
 
@@ -215,17 +215,20 @@ def tile_list_bilinear_koopman_step_kernel(
         for e in range(4):
             rows = tab_scales[:, e :: 4, :].rearrange("a q c -> q a c")
             nc.sync.dma_start(tab_sc[e:P:16, :].bitcast(I32), rows.bitcast(I32))
-        nc.sync.dma_start(wb_wd_raw[:].bitcast(I32), wb_words.rearrange("a p c -> p a c").bitcast(I32))
         wa_raw = {(0, 0): load_wa(0, 0, 2)}
         load_scale_rows(wb_sc_raw, wb_scales)
+        for b in range(BLOCKS):
+            rows = wb_words[:, :, 2 * PASS * b : 2 * PASS * (b + 1)].rearrange("a p c -> p a c")
+            nc.sync.dma_start(wb_wd_raw[b][:].bitcast(I32), rows.bitcast(I32))
         wa_raw[0, 1] = load_wa(0, 1, 0)
         gather_words(0)
         nc.vector.tensor_copy(v_sc[0][:], tab_sc[:].indirect(offsets[:]))
         nc.sync.dma_start(v_sc[1][0 : P - 16, :].bitcast(I32), v_sc[0][16:P, :].bitcast(I32))
         gather_words(1)
         g_raw = {(0, 0): load_g(0, 0, 4)}
-        for b in range(BLOCKS):
-            reorder_wb(b)
+        reorder_wb(0)
+        wb_sc.append(keep.tile([P, PACK, PASSES, P], U8, name="wb_sc1", tag="wb_wd_raw0", align_bytes=64))
+        reorder_wb(1)
 
         g_raw[0, 1] = load_g(0, 1, 1)
         nc.sync.dma_start(drift_col[:], drift.rearrange("(b p t) -> p b t", b=BLOCKS, t=PACK))
@@ -249,18 +252,24 @@ def tile_list_bilinear_koopman_step_kernel(
             nc.sync.dma_start(xop_col[:], xop.rearrange("(c p) -> p c", p=P))
         for lo, hi in HALVES:
             gate(0, 0, lo, hi)
-        for t in range(1, PACK):
+        for t in range(1, PACK - 1):
             gate(0, t, 0, S)
-        add_h(0, 0, S)
+        for lo, hi in HALVES:
+            gate(0, PACK - 1, lo, hi)
+        for lo, hi in HALVES:
+            add_h(0, lo, hi)
 
         for a in range(PASSES):
             round_wa(1, a)
         quantize(flat(wa_wd[1]), flat(wa_sc[1]), flat(wa_bf[1]))
         wb_prod.append(product_wb(1))
         gate(1, 0, 0, S)
-        quantize_h(0, 0, S)
-        for t in range(1, PACK):
+        for lo, hi in HALVES:
+            quantize_h(0, lo, hi)
+        for t in range(1, PACK - 1):
             gate(1, t, 0, S)
+        for lo, hi in HALVES:
+            gate(1, PACK - 1, lo, hi)
         product_wa(1)
         wc_bf = keep.tile([P, BLOCKS, PACK * N], BF16, name="wc_bf", tag="wa_wd1", align_bytes=64)
         for b in range(BLOCKS):
@@ -271,7 +280,7 @@ def tile_list_bilinear_koopman_step_kernel(
             if n + 1 < len(PIECES):
                 add_h(1, *PIECES[n + 1])
             if n == 0:
-                wc_wd = keep.tile([P, BLOCKS, N], U32, name="wc_wd", tag="auto_last0", align_bytes=64)
+                wc_wd = mx_tile("wc_wd", [BLOCKS, N], U32)
                 quantize(flat(wc_wd), flat(wc_sc), flat(wc_bf))
                 h_wd.append(keep.tile([P, S], U32, name="h_wd1", tag="wa_wd1", align_bytes=64))
             quantize_h(1, lo, hi)

@@ -29,7 +29,7 @@ BANK = 512
 HALVES = [(lo, lo + BANK) for lo in range(0, S, BANK)]
 PIECE = 256
 PIECES = [(lo, lo + PIECE) for lo in range(0, S - PIECE, PIECE)] + [(lo, lo + PIECE // 2) for lo in range(S - PIECE, S, PIECE // 2)]
-STREAM_BUFS = 5
+STREAM_BUFS = 6
 BUF_BYTES = 4 * T
 
 
@@ -74,7 +74,6 @@ def tile_list_bilinear_koopman_step_kernel(
         auto_last = [mx_tile(f"auto_last{u}", [PACK, BANK], F32) for u in range(len(HALVES))]
         result = keep.tile([P, OUT_TILES * S], F32, name="result")
         drift_col = keep.tile([P, BLOCKS, PACK], F32, name="drift_col")
-        xop_col = keep.tile([P, OUT_TILES], F32, name="xop_col", tag="wa_wd0", align_bytes=64)
 
         def load_table_words(a):
             nc.sync.dma_start(tab_wd[a][:], tab_words[a].rearrange("p t i -> p (t i)").bitcast(I32))
@@ -95,6 +94,10 @@ def tile_list_bilinear_koopman_step_kernel(
             tile = large(buf, [BLOCKS, PACK * N], F32)
             nc.sync.dma_start(tile[:], wc.rearrange("(b p t) n -> p b (t n)", b=BLOCKS, t=PACK))
             return tile
+
+        def load_wb_words(b):
+            rows = wb_words[:, :, 2 * PASS * b : 2 * PASS * (b + 1)].rearrange("a p c -> p a c")
+            nc.sync.dma_start(wb_wd_raw[b][:].bitcast(I32), rows.bitcast(I32))
 
         def load_scale_rows(tile, src):
             for e in range(4):
@@ -148,15 +151,14 @@ def tile_list_bilinear_koopman_step_kernel(
                 mx_pass(acc, n, len(operands), *operand)
             return acc
 
-        def product_wb(b):
-            prod = b_pool.tile([P, PACK, S], F32, name=f"prod{b}")
+        def product_wb(b, prod):
             for t in range(PACK):
                 for lo, hi in HALVES:
                     passes = [
                         (wb_wd[b][:, t, a, :].bitcast(FP4X4), wb_sc[b][:, t, a, :], v_wd[a][:, lo:hi], v_sc[a][:, lo:hi])
                         for a in reversed(range(PASSES))
                     ]
-                    nc.scalar.copy(prod[:, t, lo:hi], mx_sum(BANK, passes)[:])
+                    nc.scalar.copy(prod[t][:, lo:hi], mx_sum(BANK, passes)[:])
             return prod
 
         def auto_part(b, lo, hi):
@@ -177,7 +179,7 @@ def tile_list_bilinear_koopman_step_kernel(
 
         def gate(b, t, lo, hi):
             window = g_raw[b, t][:].indirect(listed(lo, hi))
-            nc.vector.tensor_tensor(gated[b][:, t, lo:hi], window, wb_prod[b][:, t, lo:hi], MULT)
+            nc.vector.tensor_tensor(gated[b][:, t, lo:hi], window, wb_prod[b][t][:, lo:hi], MULT)
 
         def add_h(b, lo, hi):
             name = f"h_bf{b}"
@@ -217,15 +219,14 @@ def tile_list_bilinear_koopman_step_kernel(
             nc.sync.dma_start(tab_sc[e:P:16, :].bitcast(I32), rows.bitcast(I32))
         wa_raw = {(0, 0): load_wa(0, 0, 2)}
         load_scale_rows(wb_sc_raw, wb_scales)
-        for b in range(BLOCKS):
-            rows = wb_words[:, :, 2 * PASS * b : 2 * PASS * (b + 1)].rearrange("a p c -> p a c")
-            nc.sync.dma_start(wb_wd_raw[b][:].bitcast(I32), rows.bitcast(I32))
-        wa_raw[0, 1] = load_wa(0, 1, 0)
+        load_wb_words(0)
+        wa_raw[0, 1] = load_wa(0, 1, 4)
+        load_wb_words(1)
         gather_words(0)
         nc.vector.tensor_copy(v_sc[0][:], tab_sc[:].indirect(offsets[:]))
         nc.sync.dma_start(v_sc[1][0 : P - 16, :].bitcast(I32), v_sc[0][16:P, :].bitcast(I32))
         gather_words(1)
-        g_raw = {(0, 0): load_g(0, 0, 4)}
+        g_raw = {(0, 0): load_g(0, 0, 5)}
         reorder_wb(0)
         wb_sc.append(keep.tile([P, PACK, PASSES, P], U8, name="wb_sc1", tag="wb_wd_raw0", align_bytes=64))
         reorder_wb(1)
@@ -233,23 +234,22 @@ def tile_list_bilinear_koopman_step_kernel(
         g_raw[0, 1] = load_g(0, 1, 1)
         nc.sync.dma_start(drift_col[:], drift.rearrange("(b p t) -> p b t", b=BLOCKS, t=PACK))
         g_raw[0, 2] = load_g(0, 2, 2)
-        g_raw[0, 3] = load_g(0, 3, 0)
+        g_raw[0, 3] = load_g(0, 3, 4)
 
         round_wa(0, 0)
         quantize(wa_wd[0][:, 0, :], wa_sc[0][:, 0, :], wa_bf[0][:, 0, :])
         round_wa(0, 1)
         quantize(wa_wd[0][:, 1, :], wa_sc[0][:, 1, :], wa_bf[0][:, 1, :])
         wa_raw[1, 0] = load_wa(1, 0, 3)
-        g_raw[1, 0] = load_g(1, 0, 4)
+        g_raw[1, 0] = load_g(1, 0, 5)
         wa_raw[1, 1] = load_wa(1, 1, 1)
         g_raw[1, 1] = load_g(1, 1, 2)
-        g_raw[1, 2] = load_g(1, 2, 0)
-        g_raw[1, 3] = load_g(1, 3, 3)
-        wc_raw = load_wc(4)
-        wb_prod = [product_wb(0)]
+        g_raw[1, 2] = load_g(1, 2, 4)
+        early, late = b_pool.tile([P, 2, S], F32, name="prod0"), large(0, [2, S], F32)
+        wb_prod = [product_wb(0, [early[:, 0, :], early[:, 1, :], late[:, 0, :], late[:, 1, :]])]
+        g_raw[1, 3] = load_g(1, 3, 0)
+        wc_raw = load_wc(5)
         product_wa(0)
-        with nc.allow_non_contiguous_dma(reason="one bias value a partition"):
-            nc.sync.dma_start(xop_col[:], xop.rearrange("(c p) -> p c", p=P))
         for lo, hi in HALVES:
             gate(0, 0, lo, hi)
         for t in range(1, PACK - 1):
@@ -259,10 +259,15 @@ def tile_list_bilinear_koopman_step_kernel(
         for lo, hi in HALVES:
             add_h(0, lo, hi)
 
+        xop_col = b_pool.tile([P, OUT_TILES], F32, name="xop_col", tag="prod0")
+        with nc.allow_non_contiguous_dma(reason="one bias value a partition"):
+            nc.sync.dma_start(xop_col[:], xop.rearrange("(c p) -> p c", p=P))
+
         for a in range(PASSES):
             round_wa(1, a)
         quantize(flat(wa_wd[1]), flat(wa_sc[1]), flat(wa_bf[1]))
-        wb_prod.append(product_wb(1))
+        first, middle, last = b_pool.tile([P, S], F32, name="prod1"), large(3, [2, S], F32), large(1, [S], F32)
+        wb_prod.append(product_wb(1, [first[:], middle[:, 0, :], middle[:, 1, :], last[:]]))
         gate(1, 0, 0, S)
         for lo, hi in HALVES:
             quantize_h(0, lo, hi)

@@ -1,6 +1,7 @@
 from contextlib import ExitStack
 
 import concourse.mybir as mybir
+from concourse.masks import make_identity
 
 K, T, S, H, N = 1024, 2048, 1024, 1024, 256
 FLOPS = 2 * K * H * S * 2 + 2 * H * N * S
@@ -25,6 +26,7 @@ BLOCKS = H // PASS
 OUT_TILES = N // P
 QUADS = 4
 GROUP = 16
+BANKS = 8
 BANK = 512
 HALVES = [(lo, lo + BANK) for lo in range(0, S, BANK)]
 PIECE = 256
@@ -43,7 +45,15 @@ def tile_list_bilinear_koopman_step_kernel(
         b_pool = ctx.enter_context(tc.tile_pool(name="b_pool", bufs=1))
         h_pool = ctx.enter_context(tc.tile_pool(name="h_pool", bufs=1))
         h_bf = {}
-        psum = ctx.enter_context(tc.psum_pool(name="psum", bufs=8))
+        psum = ctx.enter_context(tc.psum_pool(name="psum", bufs=1))
+        taken = []
+
+        def bank(shape, number=None):
+            taken.append((taken[-1] + 1) % BANKS if number is None else number)
+            name = f"acc{len(taken)}"
+            return psum.tile([P, *shape], F32, name=name, tag=name, offset=4 * BANK * taken[-1])
+
+        taken.append(-1)
 
         def mx_tile(name, shape, dtype):
             return keep.tile([P, *shape], dtype, name=name, tag=name, align_bytes=64)
@@ -63,11 +73,17 @@ def tile_list_bilinear_koopman_step_kernel(
         wb_wd = [mx_tile(f"wb_wd{b}", [PACK, PASSES, 2 * P], U8) for b in range(BLOCKS)]
         wb_sc = [mx_tile("wb_sc0", [PACK, PASSES, P], U8)]
         v_sc = [mx_tile(f"v_sc{a}", [S], U8) for a in range(PASSES)]
-        wa_wd = [mx_tile(f"wa_wd{b}", [PASSES, PASS], U32) for b in range(BLOCKS)]
+        spare = end + 4 * S
+
+        def placed(name, offset, shape, dtype):
+            return stream.tile([P, *shape], dtype, name=name, tag=name, align_bytes=64, offset=offset)
+
+        wa_wd = [mx_tile("wa_wd0", [PASSES, PASS], U32), placed("wa_wd1", spare, [PASSES, PASS], U32)]
+        ident = keep.tile([P, P], F32, name="ident")
         wa_sc = [mx_tile(f"wa_sc{b}", [PASSES, PASS], U8) for b in range(BLOCKS)]
-        wa_bf = [large(3, [PASSES, PACK * PASS], BF16), mx_tile("wa_bf1", [PASSES, PACK * PASS], BF16)]
+        wa_bf = [large(3, [PASSES, PACK * PASS], BF16), large(7, [PASSES, PACK * PASS], BF16)]
         wc_sc = mx_tile("wc_sc", [BLOCKS, N], U8)
-        h_wd = [mx_tile("h_wd0", [S], U32)]
+        h_wd = {(0, u): mx_tile(f"h_wd0{u}", [BANK], U32) for u in range(2)}
         h_sc = [mx_tile(f"h_sc{b}", [S], U8) for b in range(BLOCKS)]
         gated = [keep.tile([P, PACK, S], F32, name=f"gated{b}") for b in range(BLOCKS)]
         auto_first = keep.tile([P, PACK, S], F32, name="auto_first")
@@ -146,19 +162,20 @@ def tile_list_bilinear_koopman_step_kernel(
             )
 
         def mx_sum(width, operands):
-            acc = psum.tile([P, width], F32, name="acc")
+            acc = bank([width])
             for n, operand in enumerate(operands):
                 mx_pass(acc, n, len(operands), *operand)
             return acc
 
-        def product_wb(b, prod):
-            for t in range(PACK):
+        def product_wb(b, prod, tiles):
+            for t in tiles:
                 for lo, hi in HALVES:
                     passes = [
                         (wb_wd[b][:, t, a, :].bitcast(FP4X4), wb_sc[b][:, t, a, :], v_wd[a][:, lo:hi], v_sc[a][:, lo:hi])
                         for a in reversed(range(PASSES))
                     ]
-                    nc.scalar.copy(prod[t][:, lo:hi], mx_sum(BANK, passes)[:])
+                    part = prod[t][lo // BANK] if isinstance(prod[t], list) else prod[t][:, lo:hi]
+                    nc.scalar.copy(part, mx_sum(BANK, passes)[:])
             return prod
 
         def auto_part(b, lo, hi):
@@ -166,8 +183,8 @@ def tile_list_bilinear_koopman_step_kernel(
                 return auto_first[:, :, lo:hi]
             return auto_last[lo // BANK][:, :, lo % BANK : lo % BANK + hi - lo]
 
-        def product_wa(b):
-            for lo, hi in HALVES:
+        def product_wa(b, halves):
+            for lo, hi in halves:
                 for t in range(PACK):
                     cols = slice(P * t, P * (t + 1))
                     passes = [
@@ -177,9 +194,13 @@ def tile_list_bilinear_koopman_step_kernel(
                     acc = mx_sum(BANK, passes)
                     nc.scalar.activation(auto_part(b, lo, hi)[:, t, :], acc[:], IDENT, bias=drift_col[:, b, t : t + 1])
 
+        def prod_part(b, t, lo, hi):
+            part = wb_prod[b][t]
+            return part[lo // BANK] if isinstance(part, list) else part[:, lo:hi]
+
         def gate(b, t, lo, hi):
             window = g_raw[b, t][:].indirect(listed(lo, hi))
-            nc.vector.tensor_tensor(gated[b][:, t, lo:hi], window, wb_prod[b][t][:, lo:hi], MULT)
+            nc.vector.tensor_tensor(gated[b][:, t, lo:hi], window, prod_part(b, t, lo, hi), MULT)
 
         def add_h(b, lo, hi):
             name = f"h_bf{b}"
@@ -187,16 +208,43 @@ def tile_list_bilinear_koopman_step_kernel(
             dst = interleaved(h_bf[b, lo][:])
             nc.vector.tensor_tensor(dst, by_pairs(auto_part(b, lo, hi)), by_pairs(gated[b][:, :, lo:hi]), ADD)
 
+        def h_words(b, lo, hi):
+            return h_wd[b, lo // BANK][:, lo % BANK : lo % BANK + hi - lo]
+
         def quantize_h(b, lo, hi):
-            quantize(h_wd[b][:, lo:hi], h_sc[b][:, lo:hi], h_bf[b, lo][:])
+            quantize(h_words(b, lo, hi), h_sc[b][:, lo:hi], h_bf[b, lo][:])
+
+        def turn_and_add(acc, b, t, lo):
+            terms = [auto_part(b, lo, lo + P)[:, t, :], gated[b][:, t, lo : lo + P]]
+            for n, term in enumerate(terms):
+                nc.tensor.matmul(acc[:, t, :], term, ident[:], start=(n == 0), stop=(n == 1), is_transpose=True)
+
+        def add_h_turned(b, lo, hi, turned):
+            units = range((hi - lo) // P)
+            accs = [bank([PACK, P]) for w in units]
+            for t in range(PACK):
+                for w in units:
+                    turn_and_add(accs[w], b, t, lo + P * w)
+            for w in units:
+                dst = turned[w][:].rearrange("p (u m e) -> p u m e", u=2, e=2)
+                nc.scalar.copy(dst, accs[w][:].rearrange("p (u e) m -> p u m e", u=2))
+            for v in range(len(units) // 2):
+                h_bf[b, lo + PIECE * v] = mx_tile(f"h_turned{v}", [PACK * PIECE], BF16)
+                words = h_bf[b, lo + PIECE * v][:].bitcast(F32).rearrange("p (w j u) -> p w j u", w=2, u=2)
+                acc = bank([2, 2, P])
+                for w in range(2):
+                    pairs = turned[2 * v + w][:].bitcast(F32)
+                    for u in range(2):
+                        nc.tensor.transpose(acc[:, w, u, :], pairs[:, P * u : P * (u + 1)], ident[:])
+                nc.scalar.copy(words, acc[:].rearrange("p w u j -> p w j u"))
 
         def decode(lo, hi):
             piece = result[:, OUT_TILES * lo : OUT_TILES * hi].rearrange("p (c j) -> p c j", c=OUT_TILES)
-            accs = [psum.tile([P, hi - lo], F32, name="acc") for c in range(OUT_TILES)]
+            accs = [bank([hi - lo]) for c in range(OUT_TILES)]
             for b in range(BLOCKS):
                 for c in range(OUT_TILES):
                     cols = slice(P * c, P * (c + 1))
-                    mx_pass(accs[c], b, BLOCKS, wc_wd[:, b, cols].bitcast(FP8X4), wc_sc[:, b, cols], h_wd[b][:, lo:hi], h_sc[b][:, lo:hi])
+                    mx_pass(accs[c], b, BLOCKS, wc_wd[:, b, cols].bitcast(FP8X4), wc_sc[:, b, cols], h_words(b, lo, hi), h_sc[b][:, lo:hi])
             rows = out[:, lo:hi].rearrange("(c p) j -> p c j", p=P)
             nc.scalar.activation(piece[:, 0, :], accs[0][:], IDENT, bias=xop_col[:, 0:1])
             if hi < S:
@@ -208,6 +256,7 @@ def tile_list_bilinear_koopman_step_kernel(
                 nc.sync.dma_start(rows[:, 1, :], piece[:, 1, :])
 
         nc.gpsimd.memset(tab_sc[:].bitcast(I32), 0)
+        make_identity(nc, ident[:])
         nc.vector.memset(wb_sc_raw[:].bitcast(I32), 0)
         nc.vector.memset(v_sc[1][:].bitcast(I32), 0)
 
@@ -241,15 +290,14 @@ def tile_list_bilinear_koopman_step_kernel(
         round_wa(0, 1)
         quantize(wa_wd[0][:, 1, :], wa_sc[0][:, 1, :], wa_bf[0][:, 1, :])
         wa_raw[1, 0] = load_wa(1, 0, 3)
-        g_raw[1, 0] = load_g(1, 0, 5)
-        wa_raw[1, 1] = load_wa(1, 1, 1)
-        g_raw[1, 1] = load_g(1, 1, 2)
-        g_raw[1, 2] = load_g(1, 2, 4)
+        wa_raw[1, 1] = load_wa(1, 1, 5)
+        wc_raw = load_wc(1)
+        g_raw[1, 0] = load_g(1, 0, 2)
+        g_raw[1, 1] = load_g(1, 1, 4)
         early, late = b_pool.tile([P, 2, S], F32, name="prod0"), large(0, [2, S], F32)
-        wb_prod = [product_wb(0, [early[:, 0, :], early[:, 1, :], late[:, 0, :], late[:, 1, :]])]
-        g_raw[1, 3] = load_g(1, 3, 0)
-        wc_raw = load_wc(5)
-        product_wa(0)
+        wb_prod = [product_wb(0, [early[:, 0, :], early[:, 1, :], late[:, 0, :], late[:, 1, :]], range(PACK))]
+        g_raw[1, 2] = load_g(1, 2, 0)
+        product_wa(0, HALVES)
         for lo, hi in HALVES:
             gate(0, 0, lo, hi)
         for t in range(1, PACK - 1):
@@ -263,30 +311,35 @@ def tile_list_bilinear_koopman_step_kernel(
         with nc.allow_non_contiguous_dma(reason="one bias value a partition"):
             nc.sync.dma_start(xop_col[:], xop.rearrange("(c p) -> p c", p=P))
 
+        for lo, hi in HALVES:
+            quantize_h(0, lo, hi)
+        wb_prod.append([b_pool.tile([P, S], F32, name="prod1")[:]])
+        product_wb(1, wb_prod[1], [0])
         for a in range(PASSES):
             round_wa(1, a)
         quantize(flat(wa_wd[1]), flat(wa_sc[1]), flat(wa_bf[1]))
-        first, middle, last = b_pool.tile([P, S], F32, name="prod1"), large(3, [2, S], F32), large(1, [S], F32)
-        wb_prod.append(product_wb(1, [first[:], middle[:, 0, :], middle[:, 1, :], last[:]]))
-        gate(1, 0, 0, S)
-        for lo, hi in HALVES:
-            quantize_h(0, lo, hi)
-        for t in range(1, PACK - 1):
-            gate(1, t, 0, S)
-        for lo, hi in HALVES:
-            gate(1, PACK - 1, lo, hi)
-        product_wa(1)
-        wc_bf = keep.tile([P, BLOCKS, PACK * N], BF16, name="wc_bf", tag="wa_wd1", align_bytes=64)
+        g_raw[1, 3] = load_g(1, 3, 7)
+        wc_bf = large(8, [BLOCKS, PACK * N], BF16)
         for b in range(BLOCKS):
             nc.scalar.copy(interleaved(wc_bf[:, b, :]), by_pairs(wc_raw[:, b, :].rearrange("p (t n) -> p t n", t=PACK)))
-
-        add_h(1, *PIECES[0])
-        for n, (lo, hi) in enumerate(PIECES):
-            if n + 1 < len(PIECES):
-                add_h(1, *PIECES[n + 1])
-            if n == 0:
-                wc_wd = mx_tile("wc_wd", [BLOCKS, N], U32)
-                quantize(flat(wc_wd), flat(wc_sc), flat(wc_bf))
-                h_wd.append(keep.tile([P, S], U32, name="h_wd1", tag="wa_wd1", align_bytes=64))
-            quantize_h(1, lo, hi)
-            decode(lo, hi)
+        wc_wd = mx_tile("wc_wd", [BLOCKS, N], U32)
+        quantize(flat(wc_wd), flat(wc_sc), flat(wc_bf))
+        middle = large(1, [2, S], F32)
+        wb_prod[1].extend([middle[:, 0, :], middle[:, 1, :], large(5, [S], F32)[:]])
+        product_wb(1, wb_prod[1], range(1, PACK))
+        product_wa(1, HALVES)
+        for t in range(PACK - 1):
+            gate(1, t, 0, S)
+        gate(1, PACK - 1, 0, PIECE)
+        gate(1, PACK - 1, PIECE, S - PIECE)
+        gate(1, PACK - 1, S - PIECE, S)
+        turned = [placed(f"turned{w}", 3 * BUF_BYTES + 2 * PASS * w, [PASS], BF16) for w in range(PIECE // P)]
+        add_h_turned(1, *PIECES[0], turned)
+        for u in range(2):
+            h_wd[1, u] = mx_tile(f"h_wd1{u}", [BANK], U32)
+        add_h(1, *PIECES[1])
+        for n, later in ((1, 2), (0, 3), (2, 4), (3, None), (4, None)):
+            if later:
+                add_h(1, *PIECES[later])
+            quantize_h(1, *PIECES[n])
+            decode(*PIECES[n])

@@ -33,6 +33,7 @@ PIECE = 256
 PIECES = [(lo, lo + PIECE) for lo in range(0, S - PIECE, PIECE)] + [(lo, lo + PIECE // 2) for lo in range(S - PIECE, S, PIECE // 2)]
 STREAM_BUFS = 6
 BUF_BYTES = 4 * T
+DMA_ALIGN = 256
 
 
 def tile_list_bilinear_koopman_step_kernel(
@@ -62,14 +63,14 @@ def tile_list_bilinear_koopman_step_kernel(
 
         def large(buf, shape, dtype):
             name = f"large{buf}"
-            return stream.tile([P, *shape], dtype, name=name, tag=name, align_bytes=64, offset=buf * BUF_BYTES)
+            return stream.tile([P, *shape], dtype, name=name, tag=name, align_bytes=DMA_ALIGN, offset=buf * BUF_BYTES)
 
         tab_wd = [large(a, [T], I32) for a in range(PASSES)]
         end = STREAM_BUFS * BUF_BYTES
         tab_sc = stream.tile([P, T], U8, name="tab_sc", align_bytes=64, offset=end - T // 2)
         v_wd = [mx_tile("v_wd0", [S], U32), stream.tile([P, S], U32, name="v_wd1", align_bytes=64, offset=end)]
         wb_sc_raw = mx_tile("wb_sc_raw", [PASSES, H], U8)
-        wb_wd_raw = [mx_tile(f"wb_wd_raw{b}", [PASSES, 2 * PASS], U8) for b in range(BLOCKS)]
+        wb_wd_raw = [keep.tile([P, PASSES, 2 * PASS], U8, name=f"wb_wd_raw{b}", align_bytes=DMA_ALIGN) for b in range(BLOCKS)]
         wb_wd = [mx_tile(f"wb_wd{b}", [PACK, PASSES, 2 * P], U8) for b in range(BLOCKS)]
         wb_sc = [mx_tile("wb_sc0", [PACK, PASSES, P], U8)]
         v_sc = [mx_tile(f"v_sc{a}", [S], U8) for a in range(PASSES)]
@@ -88,7 +89,7 @@ def tile_list_bilinear_koopman_step_kernel(
         gated = [keep.tile([P, PACK, S], F32, name=f"gated{b}") for b in range(BLOCKS)]
         auto_first = keep.tile([P, PACK, S], F32, name="auto_first")
         auto_last = [mx_tile(f"auto_last{u}", [PACK, BANK], F32) for u in range(len(HALVES))]
-        result = keep.tile([P, OUT_TILES * S], F32, name="result")
+        result = keep.tile([P, OUT_TILES * S], F32, name="result", align_bytes=DMA_ALIGN)
         drift_col = keep.tile([P, BLOCKS, PACK], F32, name="drift_col")
 
         def load_table_words(a):
@@ -277,7 +278,7 @@ def tile_list_bilinear_koopman_step_kernel(
         gather_words(1)
         g_raw = {(0, 0): load_g(0, 0, 5)}
         reorder_wb(0)
-        wb_sc.append(keep.tile([P, PACK, PASSES, P], U8, name="wb_sc1", tag="wb_wd_raw0", align_bytes=64))
+        wb_sc.append(keep.tile([P, PACK, PASSES, P], U8, name="wb_sc1", tag="wb_wd_raw0", align_bytes=DMA_ALIGN))
         reorder_wb(1)
 
         g_raw[0, 1] = load_g(0, 1, 1)

@@ -24,15 +24,13 @@ PASS = P * PACK
 PASSES = K // PASS
 BLOCKS = H // PASS
 OUT_TILES = N // P
-QUADS = 4
 GROUP = 16
 BANKS = 8
 BANK = 512
 HALVES = [(lo, lo + BANK) for lo in range(0, S, BANK)]
 PIECE = 256
-PIECES = [(lo, lo + PIECE) for lo in range(0, S - PIECE, PIECE)] + [(lo, lo + PIECE // 2) for lo in range(S - PIECE, S, PIECE // 2)]
-STREAM_BUFS = 6
-BUF_BYTES = 4 * T
+KIB = 1024
+BUF = 8 * KIB
 DMA_ALIGN = 256
 
 
@@ -43,94 +41,73 @@ def tile_list_bilinear_koopman_step_kernel(
     with ExitStack() as ctx:
         keep = ctx.enter_context(tc.tile_pool(name="keep", bufs=1))
         stream = ctx.enter_context(tc.tile_pool(name="stream", bufs=1))
-        b_pool = ctx.enter_context(tc.tile_pool(name="b_pool", bufs=1))
-        h_pool = ctx.enter_context(tc.tile_pool(name="h_pool", bufs=1))
-        h_bf = {}
+        ring = ctx.enter_context(tc.tile_pool(name="ring", bufs=1))
         psum = ctx.enter_context(tc.psum_pool(name="psum", bufs=1))
-        taken = []
+        banks_taken = []
 
-        def bank(shape, number=None):
-            taken.append((taken[-1] + 1) % BANKS if number is None else number)
-            name = f"acc{len(taken)}"
-            return psum.tile([P, *shape], F32, name=name, tag=name, offset=4 * BANK * taken[-1])
-
-        taken.append(-1)
+        def bank(number, shape):
+            banks_taken.append(number)
+            name = f"acc{len(banks_taken)}"
+            return psum.tile([P, *shape], F32, name=name, tag=name, offset=4 * BANK * number)
 
         def mx_tile(name, shape, dtype):
             return keep.tile([P, *shape], dtype, name=name, tag=name, align_bytes=64)
 
-        offsets = keep.tile([P, S // GROUP], U16, name="offsets")
-
-        def large(buf, shape, dtype):
-            name = f"large{buf}"
-            return stream.tile([P, *shape], dtype, name=name, tag=name, align_bytes=DMA_ALIGN, offset=buf * BUF_BYTES)
-
-        tab_wd = [large(a, [T], I32) for a in range(PASSES)]
-        end = STREAM_BUFS * BUF_BYTES
-        tab_sc = stream.tile([P, T], U8, name="tab_sc", align_bytes=64, offset=end - T // 2)
-        v_wd = [mx_tile("v_wd0", [S], U32), stream.tile([P, S], U32, name="v_wd1", align_bytes=64, offset=end)]
-        wb_sc_raw = mx_tile("wb_sc_raw", [PASSES, H], U8)
-        wb_wd_raw = [keep.tile([P, PASSES, 2 * PASS], U8, name=f"wb_wd_raw{b}", align_bytes=DMA_ALIGN) for b in range(BLOCKS)]
-        wb_wd = [mx_tile(f"wb_wd{b}", [PACK, PASSES, 2 * P], U8) for b in range(BLOCKS)]
-        wb_sc = [mx_tile("wb_sc0", [PACK, PASSES, P], U8)]
-        v_sc = [mx_tile(f"v_sc{a}", [S], U8) for a in range(PASSES)]
-        spare = end + 4 * S
-
         def placed(name, offset, shape, dtype):
-            return stream.tile([P, *shape], dtype, name=name, tag=name, align_bytes=64, offset=offset)
+            return stream.tile([P, *shape], dtype, name=name, tag=name, align_bytes=DMA_ALIGN, offset=offset)
 
-        wa_wd = [mx_tile("wa_wd0", [PASSES, PASS], U32), placed("wa_wd1", spare, [PASSES, PASS], U32)]
-        ident = keep.tile([P, P], F32, name="ident")
+        offsets = keep.tile([P, S // GROUP], U16, name="offsets")
+        tab_wd = [placed(f"tab_wd{a}", a * BUF, [T], I32) for a in range(PASSES)]
+        tab_sc = placed("tab_sc", 6 * BUF - KIB, [T], U8)
+        v_wd = [mx_tile("v_wd0", [S], U32), placed("v_wd1", 6 * BUF, [S], U32)]
+        v_sc = [mx_tile(f"v_sc{a}", [S], U8) for a in range(PASSES)]
+        wb_sc_raw = mx_tile("wb_sc_raw", [PASSES, H], U8)
+        wb_wd_raw = keep.tile([P, PASSES, 2 * H], U8, name="wb_wd_raw", align_bytes=DMA_ALIGN)
+        wb_wd = [mx_tile(f"wb_wd{b}", [PACK, PASSES, 2 * P], U8) for b in range(BLOCKS)]
+        wb_sc = [mx_tile(f"wb_sc{b}", [PACK, PASSES, P], U8) for b in range(BLOCKS)]
+        wa_wd = [mx_tile(f"wa_wd{b}", [PASSES, PASS], U32) for b in range(BLOCKS)]
         wa_sc = [mx_tile(f"wa_sc{b}", [PASSES, PASS], U8) for b in range(BLOCKS)]
-        wa_bf = [large(3, [PASSES, PACK * PASS], BF16), large(7, [PASSES, PACK * PASS], BF16)]
+        first_bf = placed("wa_bf0", 3 * BUF, [PASSES, PACK * PASS], BF16)
+        wa_bf = {(0, a): first_bf[:, a, :] for a in range(PASSES)}
+        wa_bf[1, 0] = placed("wa_bf10", 7 * BUF, [PACK * PASS], BF16)[:]
+        wa_bf[1, 1] = placed("wa_bf11", 8 * BUF + 2 * KIB, [PACK * PASS], BF16)[:]
+        wc_bf = mx_tile("wc_bf", [BLOCKS, PACK * N], BF16)
+        wc_wd = mx_tile("wc_wd", [BLOCKS, N], U32)
         wc_sc = mx_tile("wc_sc", [BLOCKS, N], U8)
-        h_wd = {(0, u): mx_tile(f"h_wd0{u}", [BANK], U32) for u in range(2)}
+        h_wd = [mx_tile(f"h_wd{b}", [S], U32) for b in range(BLOCKS)]
         h_sc = [mx_tile(f"h_sc{b}", [S], U8) for b in range(BLOCKS)]
         gated = [keep.tile([P, PACK, S], F32, name=f"gated{b}") for b in range(BLOCKS)]
-        auto_first = keep.tile([P, PACK, S], F32, name="auto_first")
-        auto_last = [mx_tile(f"auto_last{u}", [PACK, BANK], F32) for u in range(len(HALVES))]
         result = keep.tile([P, OUT_TILES * S], F32, name="result", align_bytes=DMA_ALIGN)
         drift_col = keep.tile([P, BLOCKS, PACK], F32, name="drift_col")
+        ident = keep.tile([P, P], F32, name="ident")
 
         def load_table_words(a):
             nc.sync.dma_start(tab_wd[a][:], tab_words[a].rearrange("p t i -> p (t i)").bitcast(I32))
 
         def load_g(b, t, buf):
-            tile = large(buf, [T], F32)
+            tile = placed(f"g{b}{t}", buf * BUF, [T], F32)
             rows = gT[b * PASS : (b + 1) * PASS, :].rearrange("(p t) c -> p t c", t=PACK)
             nc.sync.dma_start(tile[:], rows[:, t, :])
             return tile
 
         def load_wa(b, a, buf):
-            tile = large(buf, [PACK, PASS], F32)
+            tile = placed(f"wa_raw{b}{a}", buf * BUF, [PACK, PASS], F32)
             rows = wa[a * PASS : (a + 1) * PASS, b * PASS : (b + 1) * PASS]
             nc.sync.dma_start(tile[:], rows.rearrange("(p i) c -> p i c", i=PACK))
             return tile
 
         def load_wc(buf):
-            tile = large(buf, [BLOCKS, PACK * N], F32)
+            tile = placed("wc_raw", buf * BUF, [BLOCKS, PACK * N], F32)
             nc.sync.dma_start(tile[:], wc.rearrange("(b p t) n -> p b (t n)", b=BLOCKS, t=PACK))
             return tile
-
-        def load_wb_words(b):
-            rows = wb_words[:, :, 2 * PASS * b : 2 * PASS * (b + 1)].rearrange("a p c -> p a c")
-            nc.sync.dma_start(wb_wd_raw[b][:].bitcast(I32), rows.bitcast(I32))
-
-        def load_scale_rows(tile, src):
-            for e in range(4):
-                rows = src[:, e :: 4, :].rearrange("a q c -> q a c")
-                nc.sync.dma_start(tile[e:P:32, :, :].bitcast(I32), rows.bitcast(I32))
-
-        def listed(lo, hi):
-            return offsets[:, lo // GROUP : hi // GROUP]
 
         def gather_words(a):
             nc.vector.tensor_copy(v_wd[a][:], tab_wd[a][:].bitcast(U32).indirect(offsets[:]))
 
         def reorder_wb(b):
-            words = wb_wd_raw[b][:].bitcast(U16)
+            words = wb_wd_raw[:].bitcast(U16)[:, :, b * PASS : (b + 1) * PASS]
             scales = wb_sc_raw[:, :, b * PASS : (b + 1) * PASS]
-            nc.vector.tensor_copy(wb_wd[b][:].bitcast(U16), words.rearrange("p a (m t) -> p t a m", t=PACK))
+            nc.scalar.copy(wb_wd[b][:].bitcast(U16), words.rearrange("p a (m t) -> p t a m", t=PACK))
             nc.vector.tensor_copy(wb_sc[b][:], scales.rearrange("p a (m t) -> p t a m", t=PACK))
 
         def quantize(words, scales, values):
@@ -139,122 +116,121 @@ def tile_list_bilinear_koopman_step_kernel(
         def flat(tile):
             return tile[:].rearrange("p a c -> p (a c)")
 
-        def round_wa(b, a):
-            dst = wa_bf[b][:, a, :].rearrange("p (s u m i) -> p s m i u", s=2, u=2, i=PACK)
+        def round_wa(b, a, second=nc.scalar.copy):
+            dst = wa_bf[b, a].rearrange("p (s u m i) -> p s m i u", s=2, u=2, i=PACK)
             src = wa_raw[b, a][:].rearrange("p i (m s u) -> p s m i u", s=2, u=2)
-            for s in range(2):
-                nc.scalar.copy(dst[:, s], src[:, s])
+            for s, copy in enumerate((nc.scalar.copy, second)):
+                copy(dst[:, s], src[:, s])
+            quantize(wa_wd[b][:, a, :], wa_sc[b][:, a, :], wa_bf[b, a])
 
-        def interleaved(ap):
-            return ap.rearrange("p (c u t) -> p c t u", u=2, t=PACK)
+        def interleaved(ap, run=2):
+            return ap.rearrange("p (c u t) -> p c t u", u=run, t=PACK)
 
-        def by_pairs(ap):
-            return ap.rearrange("p t (c u) -> p c t u", u=2)
+        def by_runs(ap, run=2):
+            return ap.rearrange("p t (c u) -> p c t u", u=run)
 
         def mx_pass(acc, n, count, lhs, lhs_sc, rhs, rhs_sc):
             nc.tensor.matmul_mx(
-                out=acc[:],
-                lhsT=lhs,
-                lhsT_scale=lhs_sc,
-                rhs=rhs.bitcast(FP8X4),
-                rhs_scale=rhs_sc,
-                start=(n == 0),
-                stop=(n == count - 1),
+                out=acc, lhsT=lhs, lhsT_scale=lhs_sc, rhs=rhs.bitcast(FP8X4), rhs_scale=rhs_sc,
+                start=(n == 0), stop=(n == count - 1),
             )
 
-        def mx_sum(width, operands):
-            acc = bank([width])
-            for n, operand in enumerate(operands):
-                mx_pass(acc, n, len(operands), *operand)
+        def product_wb(b, t, tile, first_bank):
+            for u, (lo, hi) in enumerate(HALVES):
+                acc = bank((first_bank + u) % BANKS, [BANK])
+                for n, a in enumerate(reversed(range(PASSES))):
+                    mx_pass(acc[:], n, PASSES, wb_wd[b][:, t, a, :].bitcast(FP4X4), wb_sc[b][:, t, a, :], v_wd[a][:, lo:hi], v_sc[a][:, lo:hi])
+                nc.scalar.copy(tile[:, lo:hi], acc[:])
+            wb_prod[b, t] = tile
+
+        def product_wa(acc, b, t, lo, hi):
+            cols = slice(P * t, P * (t + 1))
+            for a in range(PASSES):
+                mx_pass(acc, a, PASSES, wa_wd[b][:, a, cols].bitcast(FP8X4), wa_sc[b][:, a, cols], v_wd[a][:, lo:hi], v_sc[a][:, lo:hi])
+
+        def wa_in_psum(b, lo, number):
+            acc = bank(number, [PACK, P])
+            for t in range(PACK):
+                product_wa(acc[:, t, :], b, t, lo, lo + P)
             return acc
 
-        def product_wb(b, prod, tiles):
-            for t in tiles:
-                for lo, hi in HALVES:
-                    passes = [
-                        (wb_wd[b][:, t, a, :].bitcast(FP4X4), wb_sc[b][:, t, a, :], v_wd[a][:, lo:hi], v_sc[a][:, lo:hi])
-                        for a in reversed(range(PASSES))
-                    ]
-                    part = prod[t][lo // BANK] if isinstance(prod[t], list) else prod[t][:, lo:hi]
-                    nc.scalar.copy(part, mx_sum(BANK, passes)[:])
-            return prod
-
-        def auto_part(b, lo, hi):
-            if b == 0:
-                return auto_first[:, :, lo:hi]
-            return auto_last[lo // BANK][:, :, lo % BANK : lo % BANK + hi - lo]
-
-        def product_wa(b, halves):
-            for lo, hi in halves:
-                for t in range(PACK):
-                    cols = slice(P * t, P * (t + 1))
-                    passes = [
-                        (wa_wd[b][:, a, cols].bitcast(FP8X4), wa_sc[b][:, a, cols], v_wd[a][:, lo:hi], v_sc[a][:, lo:hi])
-                        for a in range(PASSES)
-                    ]
-                    acc = mx_sum(BANK, passes)
-                    nc.scalar.activation(auto_part(b, lo, hi)[:, t, :], acc[:], IDENT, bias=drift_col[:, b, t : t + 1])
-
-        def prod_part(b, t, lo, hi):
-            part = wb_prod[b][t]
-            return part[lo // BANK] if isinstance(part, list) else part[:, lo:hi]
+        def wa_in_sbuf(b, lo, hi, first_bank, tile):
+            share = BANK // (hi - lo)
+            for first in range(0, PACK, share):
+                acc = bank((first_bank + first // share) % BANKS, [share, hi - lo])
+                for e in range(share):
+                    product_wa(acc[:, e, :], b, first + e, lo, hi)
+                for e in range(share):
+                    t = first + e
+                    nc.scalar.activation(tile[:, t, :], acc[:, e, :], IDENT, bias=drift_col[:, b, t : t + 1])
+            return tile
 
         def gate(b, t, lo, hi):
-            window = g_raw[b, t][:].indirect(listed(lo, hi))
-            nc.vector.tensor_tensor(gated[b][:, t, lo:hi], window, prod_part(b, t, lo, hi), MULT)
+            window = g_raw[b, t][:].indirect(offsets[:, lo // GROUP : hi // GROUP])
+            nc.vector.tensor_tensor(gated[b][:, t, lo:hi], window, wb_prod[b, t][:, lo:hi], MULT)
 
-        def add_h(b, lo, hi):
-            name = f"h_bf{b}"
-            h_bf[b, lo] = h_pool.tile([P, PACK * (hi - lo)], BF16, name=name, tag=name, bufs=2, align_bytes=64)
-            dst = interleaved(h_bf[b, lo][:])
-            nc.vector.tensor_tensor(dst, by_pairs(auto_part(b, lo, hi)), by_pairs(gated[b][:, :, lo:hi]), ADD)
+        def add_drift(b, t, lo, hi):
+            tile, first = drifted[b]
+            nc.scalar.activation(tile[:, t, lo - first : hi - first], gated[b][:, t, lo:hi], IDENT, bias=drift_col[:, b, t : t + 1])
 
-        def h_words(b, lo, hi):
-            return h_wd[b, lo // BANK][:, lo % BANK : lo % BANK + hi - lo]
+        def h_piece(b, lo, hi):
+            h_bf[b, lo] = mx_tile(f"h_bf{b}_{lo}", [PACK * (hi - lo)], BF16)
+            return h_bf[b, lo]
 
-        def quantize_h(b, lo, hi):
-            quantize(h_words(b, lo, hi), h_sc[b][:, lo:hi], h_bf[b, lo][:])
+        def add_on_vector(b, piece, lo, acc):
+            tile, first = drifted[b]
+            dst = h_bf[b, piece][:, PACK * (lo - piece) : PACK * (lo - piece + P)]
+            nc.vector.tensor_tensor(interleaved(dst), by_runs(acc[:]), by_runs(tile[:, :, lo - first : lo - first + P]), ADD)
 
-        def turn_and_add(acc, b, t, lo):
-            terms = [auto_part(b, lo, lo + P)[:, t, :], gated[b][:, t, lo : lo + P]]
-            for n, term in enumerate(terms):
-                nc.tensor.matmul(acc[:, t, :], term, ident[:], start=(n == 0), stop=(n == 1), is_transpose=True)
+        def add_from_sbuf(lo, hi):
+            h_bf[1, lo] = ring.tile([P, PACK * (hi - lo)], BF16, name="h_ring", bufs=2, align_bytes=64)
+            auto = autos[lo // BANK][:, :, lo % BANK : lo % BANK + hi - lo]
+            nc.vector.tensor_tensor(interleaved(h_bf[1, lo][:]), by_runs(auto), by_runs(gated[1][:, :, lo:hi]), ADD)
 
-        def add_h_turned(b, lo, hi, turned):
-            units = range((hi - lo) // P)
-            accs = [bank([PACK, P]) for w in units]
+        def add_on_gpsimd(b, lo, hi, auto):
+            nc.gpsimd.tensor_tensor(interleaved(h_piece(b, lo, hi)[:], 4), by_runs(auto[:], 4), by_runs(gated[b][:, :, lo:hi], 4), ADD)
+
+        def add_on_tensor(b, lo, auto, first_bank):
+            units = range(PIECE // P)
+            accs = [bank(first_bank + w, [PACK, P]) for w in units]
             for t in range(PACK):
                 for w in units:
-                    turn_and_add(accs[w], b, t, lo + P * w)
+                    terms = [auto[:, t, P * w : P * (w + 1)], gated[b][:, t, lo + P * w : lo + P * (w + 1)]]
+                    for n, term in enumerate(terms):
+                        nc.tensor.matmul(accs[w][:, t, :], term, ident[:], start=(n == 0), stop=(n == 1), is_transpose=True)
+            turned = [placed(f"turned{w}", 3 * BUF + KIB * w, [PASS], BF16) for w in units]
             for w in units:
                 dst = turned[w][:].rearrange("p (u m e) -> p u m e", u=2, e=2)
                 nc.scalar.copy(dst, accs[w][:].rearrange("p (u e) m -> p u m e", u=2))
-            for v in range(len(units) // 2):
-                h_bf[b, lo + PIECE * v] = mx_tile(f"h_turned{v}", [PACK * PIECE], BF16)
-                words = h_bf[b, lo + PIECE * v][:].bitcast(F32).rearrange("p (w j u) -> p w j u", w=2, u=2)
-                acc = bank([2, 2, P])
-                for w in range(2):
-                    pairs = turned[2 * v + w][:].bitcast(F32)
-                    for u in range(2):
-                        nc.tensor.transpose(acc[:, w, u, :], pairs[:, P * u : P * (u + 1)], ident[:])
-                nc.scalar.copy(words, acc[:].rearrange("p w u j -> p w j u"))
+            words = h_piece(b, lo, lo + PIECE)[:].bitcast(F32).rearrange("p (w j u) -> p w j u", w=2, u=2)
+            acc = bank((first_bank + 2) % BANKS, [2, 2, P])
+            for w in units:
+                pairs = turned[w][:].bitcast(F32)
+                for u in range(2):
+                    nc.tensor.transpose(acc[:, w, u, :], pairs[:, P * u : P * (u + 1)], ident[:])
+            nc.scalar.copy(words, acc[:].rearrange("p w u j -> p w j u"))
 
-        def decode(lo, hi):
+        def quantize_h(b, lo, hi):
+            quantize(h_wd[b][:, lo:hi], h_sc[b][:, lo:hi], h_bf[b, lo][:])
+
+        def decode(lo, hi, first_bank, last):
             piece = result[:, OUT_TILES * lo : OUT_TILES * hi].rearrange("p (c j) -> p c j", c=OUT_TILES)
-            accs = [bank([hi - lo]) for c in range(OUT_TILES)]
+            accs = [bank((first_bank + c) % BANKS, [hi - lo]) for c in range(OUT_TILES)]
             for b in range(BLOCKS):
                 for c in range(OUT_TILES):
                     cols = slice(P * c, P * (c + 1))
-                    mx_pass(accs[c], b, BLOCKS, wc_wd[:, b, cols].bitcast(FP8X4), wc_sc[:, b, cols], h_words(b, lo, hi), h_sc[b][:, lo:hi])
+                    mx_pass(accs[c][:], b, BLOCKS, wc_wd[:, b, cols].bitcast(FP8X4), wc_sc[:, b, cols], h_wd[b][:, lo:hi], h_sc[b][:, lo:hi])
             rows = out[:, lo:hi].rearrange("(c p) j -> p c j", p=P)
             nc.scalar.activation(piece[:, 0, :], accs[0][:], IDENT, bias=xop_col[:, 0:1])
-            if hi < S:
-                nc.scalar.activation(piece[:, 1, :], accs[1][:], IDENT, bias=xop_col[:, 1:2])
-                nc.sync.dma_start(rows, piece)
-            else:
+            if last:
                 nc.vector.tensor_scalar_add(piece[:, 1, :], accs[1][:], xop_col[:, 1:2])
                 nc.scalar.dma_start(rows[:, 0, :], piece[:, 0, :])
                 nc.sync.dma_start(rows[:, 1, :], piece[:, 1, :])
+            else:
+                nc.scalar.activation(piece[:, 1, :], accs[1][:], IDENT, bias=xop_col[:, 1:2])
+                nc.sync.dma_start(rows, piece)
+
+        wb_prod, h_bf, drifted = {}, {}, {}
 
         nc.gpsimd.memset(tab_sc[:].bitcast(I32), 0)
         make_identity(nc, ident[:])
@@ -262,85 +238,87 @@ def tile_list_bilinear_koopman_step_kernel(
         nc.vector.memset(v_sc[1][:].bitcast(I32), 0)
 
         nc.sync.dma_start(offsets[:], offs)
-        for a in range(PASSES):
-            load_table_words(a)
+        load_table_words(0)
         for e in range(4):
-            rows = tab_scales[:, e :: 4, :].rearrange("a q c -> q a c")
+            rows = tab_scales[:, e::4, :].rearrange("a q c -> q a c")
             nc.sync.dma_start(tab_sc[e:P:16, :].bitcast(I32), rows.bitcast(I32))
-        wa_raw = {(0, 0): load_wa(0, 0, 2)}
-        load_scale_rows(wb_sc_raw, wb_scales)
-        load_wb_words(0)
-        wa_raw[0, 1] = load_wa(0, 1, 4)
-        load_wb_words(1)
+        nc.sync.dma_start(wb_wd_raw[:].bitcast(I32), wb_words.rearrange("a p c -> p a c").bitcast(I32))
+        load_table_words(1)
+        for e in range(4):
+            rows = wb_scales[:, e::4, :].rearrange("a q c -> q a c")
+            nc.sync.dma_start(wb_sc_raw[e:P:32, :, :].bitcast(I32), rows.bitcast(I32))
+        wa_raw = {(0, a): load_wa(0, a, 2 + 2 * a) for a in range(PASSES)}
         gather_words(0)
         nc.vector.tensor_copy(v_sc[0][:], tab_sc[:].indirect(offsets[:]))
         nc.sync.dma_start(v_sc[1][0 : P - 16, :].bitcast(I32), v_sc[0][16:P, :].bitcast(I32))
         gather_words(1)
         g_raw = {(0, 0): load_g(0, 0, 5)}
-        reorder_wb(0)
-        wb_sc.append(keep.tile([P, PACK, PASSES, P], U8, name="wb_sc1", tag="wb_wd_raw0", align_bytes=DMA_ALIGN))
-        reorder_wb(1)
-
+        for b in range(BLOCKS):
+            reorder_wb(b)
         g_raw[0, 1] = load_g(0, 1, 1)
         nc.sync.dma_start(drift_col[:], drift.rearrange("(b p t) -> p b t", b=BLOCKS, t=PACK))
         g_raw[0, 2] = load_g(0, 2, 2)
         g_raw[0, 3] = load_g(0, 3, 4)
 
         round_wa(0, 0)
-        quantize(wa_wd[0][:, 0, :], wa_sc[0][:, 0, :], wa_bf[0][:, 0, :])
-        round_wa(0, 1)
-        quantize(wa_wd[0][:, 1, :], wa_sc[0][:, 1, :], wa_bf[0][:, 1, :])
+        round_wa(0, 1, nc.vector.tensor_copy)
         wa_raw[1, 0] = load_wa(1, 0, 3)
         wa_raw[1, 1] = load_wa(1, 1, 5)
-        wc_raw = load_wc(1)
-        g_raw[1, 0] = load_g(1, 0, 2)
-        g_raw[1, 1] = load_g(1, 1, 4)
-        early, late = b_pool.tile([P, 2, S], F32, name="prod0"), large(0, [2, S], F32)
-        wb_prod = [product_wb(0, [early[:, 0, :], early[:, 1, :], late[:, 0, :], late[:, 1, :]], range(PACK))]
-        g_raw[1, 2] = load_g(1, 2, 0)
-        product_wa(0, HALVES)
+        g_raw[1, 0] = load_g(1, 0, 1)
+        g_raw[1, 1] = load_g(1, 1, 2)
+        g_raw[1, 2] = load_g(1, 2, 4)
+        early, late = keep.tile([P, 2, S], F32, name="prod_early"), placed("prod_late", 0, [2, S], F32)
+        for t in range(PACK):
+            product_wb(0, t, (early, late)[t // 2][:, t % 2, :], 2 * t)
+        product_wb(1, 0, keep.tile([P, S], F32, name="prod10")[:], 0)
+        split = S - PIECE
+        auto = wa_in_sbuf(0, split, S, BANKS - 2, keep.tile([P, PACK, PIECE], F32, name="auto0"))
+        kept = [wa_in_psum(0, lo, lo // P) for lo in range(0, split, P)]
+        drifted[0] = (keep.tile([P, PACK, split], F32, name="drifted0"), 0)
         for lo, hi in HALVES:
             gate(0, 0, lo, hi)
+        add_drift(0, 0, 0, split)
         for t in range(1, PACK - 1):
             gate(0, t, 0, S)
-        for lo, hi in HALVES:
+            add_drift(0, t, 0, split)
+        parts = [(0, split // 2), (split // 2, split)]
+        for lo, hi in parts:
             gate(0, PACK - 1, lo, hi)
-        for lo, hi in HALVES:
-            add_h(0, lo, hi)
+            add_drift(0, PACK - 1, lo, hi)
+        gate(0, PACK - 1, split, S)
+        for first, end in parts:
+            h_piece(0, first, end)
+            for lo in range(first, end, P):
+                add_on_vector(0, first, lo, kept[lo // P])
+        add_on_gpsimd(0, split, S, auto)
+        wc_raw = load_wc(0)
+        for lo, hi in (parts[0], (split, S), parts[1]):
+            quantize_h(0, lo, hi)
 
-        xop_col = b_pool.tile([P, OUT_TILES], F32, name="xop_col", tag="prod0")
+        round_wa(1, 0)
+        round_wa(1, 1)
+        g_raw[1, 3] = load_g(1, 3, 7)
+        middle = placed("prod_middle", 5 * BUF, [2, S], F32)
+        product_wb(1, 1, middle[:, 0, :], 0)
+        product_wb(1, 2, middle[:, 1, :], 2)
+        product_wb(1, 3, placed("prod13", 8 * BUF, [S], F32)[:], 4)
+        autos = [wa_in_sbuf(1, *HALVES[0], 6, keep.tile([P, PACK, BANK], F32, name="auto10"))]
+        for b in range(BLOCKS):
+            nc.scalar.copy(interleaved(wc_bf[:, b, :]), by_runs(wc_raw[:, b, :].rearrange("p (t n) -> p t n", t=PACK)))
+        quantize(flat(wc_wd), flat(wc_sc), flat(wc_bf))
+        autos.append(wa_in_sbuf(1, *HALVES[1], 2, placed("auto11", 0, [PACK, BANK], F32)))
+        xop_col = placed("xop_col", 2 * BUF, [OUT_TILES], F32)
         with nc.allow_non_contiguous_dma(reason="one bias value a partition"):
             nc.sync.dma_start(xop_col[:], xop.rearrange("(c p) -> p c", p=P))
-
-        for lo, hi in HALVES:
-            quantize_h(0, lo, hi)
-        wb_prod.append([b_pool.tile([P, S], F32, name="prod1")[:]])
-        product_wb(1, wb_prod[1], [0])
-        for a in range(PASSES):
-            round_wa(1, a)
-        quantize(flat(wa_wd[1]), flat(wa_sc[1]), flat(wa_bf[1]))
-        g_raw[1, 3] = load_g(1, 3, 7)
-        wc_bf = large(8, [BLOCKS, PACK * N], BF16)
-        for b in range(BLOCKS):
-            nc.scalar.copy(interleaved(wc_bf[:, b, :]), by_pairs(wc_raw[:, b, :].rearrange("p (t n) -> p t n", t=PACK)))
-        wc_wd = mx_tile("wc_wd", [BLOCKS, N], U32)
-        quantize(flat(wc_wd), flat(wc_sc), flat(wc_bf))
-        middle = large(1, [2, S], F32)
-        wb_prod[1].extend([middle[:, 0, :], middle[:, 1, :], large(5, [S], F32)[:]])
-        product_wb(1, wb_prod[1], range(1, PACK))
-        product_wa(1, HALVES)
         for t in range(PACK - 1):
             gate(1, t, 0, S)
-        gate(1, PACK - 1, 0, PIECE)
-        gate(1, PACK - 1, PIECE, S - PIECE)
-        gate(1, PACK - 1, S - PIECE, S)
-        turned = [placed(f"turned{w}", 3 * BUF_BYTES + 2 * PASS * w, [PASS], BF16) for w in range(PIECE // P)]
-        add_h_turned(1, *PIECES[0], turned)
-        for u in range(2):
-            h_wd[1, u] = mx_tile(f"h_wd1{u}", [BANK], U32)
-        add_h(1, *PIECES[1])
-        for n, later in ((1, 2), (0, 3), (2, 4), (3, None), (4, None)):
+        for lo, hi in ((0, PIECE), (PIECE, S - PIECE), (S - PIECE, S)):
+            gate(1, PACK - 1, lo, hi)
+        add_on_tensor(1, 0, autos[0], 6)
+        pieces = [(0, 256), (256, 512), (512, 768), (768, 896), (896, 1024)]
+        add_from_sbuf(*pieces[1])
+        for n, (now, later) in enumerate(((1, 2), (0, 3), (2, 4), (3, None), (4, None))):
             if later:
-                add_h(1, *PIECES[later])
-            quantize_h(1, *PIECES[n])
-            decode(*PIECES[n])
+                add_from_sbuf(*pieces[later])
+            quantize_h(1, *pieces[now])
+            decode(*pieces[now], 1 + 2 * n, now == 4)

@@ -59,7 +59,7 @@ def tile_list_bilinear_koopman_step_kernel(
         offsets = keep.tile([P, S // GROUP], U16, name="offsets")
         tab_wd = [placed(f"tab_wd{a}", a * BUF, [T], I32) for a in range(PASSES)]
         tab_sc = placed("tab_sc", 6 * BUF - KIB, [T], U8)
-        v_wd = [mx_tile("v_wd0", [S], U32), placed("v_wd1", 6 * BUF, [S], U32)]
+        v_wd = [mx_tile("v_wd0", [S], U32), mx_tile("v_wd1", [S], U32)]
         v_sc = [mx_tile(f"v_sc{a}", [S], U8) for a in range(PASSES)]
         wb_sc_raw = mx_tile("wb_sc_raw", [PASSES, H], U8)
         wb_wd_raw = keep.tile([P, PASSES, 2 * H], U8, name="wb_wd_raw", align_bytes=DMA_ALIGN)
@@ -135,9 +135,9 @@ def tile_list_bilinear_koopman_step_kernel(
                 start=(n == 0), stop=(n == count - 1),
             )
 
-        def product_wb(b, t, tile, first_bank):
-            for u, (lo, hi) in enumerate(HALVES):
-                acc = bank((first_bank + u) % BANKS, [BANK])
+        def product_wb(b, t, tile, first_bank, parts=HALVES):
+            for u, (lo, hi) in enumerate(parts):
+                acc = bank((first_bank + u) % BANKS, [hi - lo])
                 for n, a in enumerate(reversed(range(PASSES))):
                     mx_pass(acc[:], n, PASSES, wb_wd[b][:, t, a, :].bitcast(FP4X4), wb_sc[b][:, t, a, :], v_wd[a][:, lo:hi], v_sc[a][:, lo:hi])
                 nc.scalar.copy(tile[:, lo:hi], acc[:])
@@ -235,7 +235,6 @@ def tile_list_bilinear_koopman_step_kernel(
         nc.gpsimd.memset(tab_sc[:].bitcast(I32), 0)
         make_identity(nc, ident[:])
         nc.vector.memset(wb_sc_raw[:].bitcast(I32), 0)
-        nc.vector.memset(v_sc[1][:].bitcast(I32), 0)
 
         nc.sync.dma_start(offsets[:], offs)
         load_table_words(0)
@@ -250,7 +249,8 @@ def tile_list_bilinear_koopman_step_kernel(
         wa_raw = {(0, a): load_wa(0, a, 2 + 2 * a) for a in range(PASSES)}
         gather_words(0)
         nc.vector.tensor_copy(v_sc[0][:], tab_sc[:].indirect(offsets[:]))
-        nc.sync.dma_start(v_sc[1][0 : P - 16, :].bitcast(I32), v_sc[0][16:P, :].bitcast(I32))
+        for e in range(4):
+            nc.sync.dma_start(v_sc[1][e:P:32, :].bitcast(I32), v_sc[0][16 + e : P : 32, :].bitcast(I32))
         gather_words(1)
         g_raw = {(0, 0): load_g(0, 0, 5)}
         for b in range(BLOCKS):
@@ -268,14 +268,16 @@ def tile_list_bilinear_koopman_step_kernel(
         g_raw[1, 1] = load_g(1, 1, 2)
         g_raw[1, 2] = load_g(1, 2, 4)
         early, late = keep.tile([P, 2, S], F32, name="prod_early"), placed("prod_late", 0, [2, S], F32)
-        for t in range(PACK):
-            product_wb(0, t, (early, late)[t // 2][:, t % 2, :], 2 * t)
-        product_wb(1, 0, keep.tile([P, S], F32, name="prod10")[:], 0)
+        first_parts = [(0, PIECE), (PIECE, BANK), (BANK, S)]
+        product_wb(0, 0, early[:, 0, :], 0, first_parts)
+        for t in range(1, PACK):
+            product_wb(0, t, (early, late)[t // 2][:, t % 2, :], 1 + 2 * t)
+        product_wb(1, 0, keep.tile([P, S], F32, name="prod10")[:], 1)
         split = S - PIECE
         auto = wa_in_sbuf(0, split, S, BANKS - 2, keep.tile([P, PACK, PIECE], F32, name="auto0"))
         kept = [wa_in_psum(0, lo, lo // P) for lo in range(0, split, P)]
         drifted[0] = (keep.tile([P, PACK, split], F32, name="drifted0"), 0)
-        for lo, hi in HALVES:
+        for lo, hi in first_parts:
             gate(0, 0, lo, hi)
         add_drift(0, 0, 0, split)
         for t in range(1, PACK - 1):

@@ -78,7 +78,6 @@ def tile_list_bilinear_koopman_step_kernel(
         h_sc = [mx_tile(f"h_sc{b}", [S], U8) for b in range(BLOCKS)]
         gated = [keep.tile([P, PACK, S], F32, name=f"gated{b}") for b in range(BLOCKS)]
         result = keep.tile([P, OUT_TILES * S], F32, name="result", align_bytes=DMA_ALIGN)
-        drift_col = keep.tile([P, BLOCKS, PACK], F32, name="drift_col")
         ident = keep.tile([P, P], F32, name="ident")
 
         def load_table_words(a):
@@ -236,8 +235,8 @@ def tile_list_bilinear_koopman_step_kernel(
         make_identity(nc, ident[:])
         nc.vector.memset(wb_sc_raw[:].bitcast(I32), 0)
 
-        nc.sync.dma_start(offsets[:], offs)
         load_table_words(0)
+        nc.sync.dma_start(offsets[:], offs)
         for e in range(4):
             rows = tab_scales[:, e::4, :].rearrange("a q c -> q a c")
             nc.sync.dma_start(tab_sc[e:P:16, :].bitcast(I32), rows.bitcast(I32))
@@ -255,8 +254,9 @@ def tile_list_bilinear_koopman_step_kernel(
         g_raw = {(0, 0): load_g(0, 0, 5)}
         for b in range(BLOCKS):
             reorder_wb(b)
-        g_raw[0, 1] = load_g(0, 1, 1)
+        drift_col = placed("drift_col", 6 * BUF, [BLOCKS, PACK], F32)
         nc.sync.dma_start(drift_col[:], drift.rearrange("(b p t) -> p b t", b=BLOCKS, t=PACK))
+        g_raw[0, 1] = load_g(0, 1, 1)
         g_raw[0, 2] = load_g(0, 2, 2)
         g_raw[0, 3] = load_g(0, 3, 4)
 

from contextlib import ExitStack

import concourse.mybir as mybir
from concourse.masks import make_identity

K, T, S, H, N = 1024, 2048, 1024, 1024, 256
FLOPS = 2 * K * H * S * 2 + 2 * H * N * S

F32 = mybir.dt.float32
BF16 = mybir.dt.bfloat16
I32 = mybir.dt.int32
U32 = mybir.dt.uint32
U16 = mybir.dt.uint16
U8 = mybir.dt.uint8
FP8X4 = mybir.dt.float8_e4m3fn_x4
FP4X4 = mybir.dt.float4_e2m1fn_x4
IDENT = mybir.ActivationFunctionType.Identity
MULT = mybir.AluOpType.mult
ADD = mybir.AluOpType.add

P = 128
PACK = 4
PASS = P * PACK
PASSES = K // PASS
BLOCKS = H // PASS
OUT_TILES = N // P
GROUP = 16
BANKS = 8
BANK = 512
HALVES = [(lo, lo + BANK) for lo in range(0, S, BANK)]
PIECE = 256
KIB = 1024
BUF = 8 * KIB
DMA_ALIGN = 256


def tile_list_bilinear_koopman_step_kernel(
    tc, tab_words, tab_scales, offs, wa, wb_words, wb_scales, gT, drift, wc, xop, out
):
    nc = tc.nc
    with ExitStack() as ctx:
        keep = ctx.enter_context(tc.tile_pool(name="keep", bufs=1))
        stream = ctx.enter_context(tc.tile_pool(name="stream", bufs=1))
        ring = ctx.enter_context(tc.tile_pool(name="ring", bufs=1))
        psum = ctx.enter_context(tc.psum_pool(name="psum", bufs=1))
        banks_taken = []

        def bank(number, shape):
            banks_taken.append(number)
            name = f"acc{len(banks_taken)}"
            return psum.tile([P, *shape], F32, name=name, tag=name, offset=4 * BANK * number)

        def mx_tile(name, shape, dtype):
            return keep.tile([P, *shape], dtype, name=name, tag=name, align_bytes=64)

        def placed(name, offset, shape, dtype):
            return stream.tile([P, *shape], dtype, name=name, tag=name, align_bytes=DMA_ALIGN, offset=offset)

        offsets = keep.tile([P, S // GROUP], U16, name="offsets")
        tab_wd = [placed(f"tab_wd{a}", a * BUF, [T], I32) for a in range(PASSES)]
        tab_sc = placed("tab_sc", 6 * BUF - KIB, [T], U8)
        v_wd = [mx_tile("v_wd0", [S], U32), mx_tile("v_wd1", [S], U32)]
        v_sc = [mx_tile(f"v_sc{a}", [S], U8) for a in range(PASSES)]
        wb_sc_raw = mx_tile("wb_sc_raw", [PASSES, H], U8)
        wb_wd_raw = keep.tile([P, PASSES, 2 * H], U8, name="wb_wd_raw", align_bytes=DMA_ALIGN)
        wb_wd = [mx_tile(f"wb_wd{b}", [PACK, PASSES, 2 * P], U8) for b in range(BLOCKS)]
        wb_sc = [mx_tile(f"wb_sc{b}", [PACK, PASSES, P], U8) for b in range(BLOCKS)]
        wa_wd = [mx_tile(f"wa_wd{b}", [PASSES, PASS], U32) for b in range(BLOCKS)]
        wa_sc = [mx_tile(f"wa_sc{b}", [PASSES, PASS], U8) for b in range(BLOCKS)]
        first_bf = placed("wa_bf0", 3 * BUF, [PASSES, PACK * PASS], BF16)
        wa_bf = {(0, a): first_bf[:, a, :] for a in range(PASSES)}
        wa_bf[1, 0] = placed("wa_bf10", 7 * BUF, [PACK * PASS], BF16)[:]
        wa_bf[1, 1] = placed("wa_bf11", 8 * BUF + 2 * KIB, [PACK * PASS], BF16)[:]
        wc_bf = mx_tile("wc_bf", [BLOCKS, PACK * N], BF16)
        wc_wd = mx_tile("wc_wd", [BLOCKS, N], U32)
        wc_sc = mx_tile("wc_sc", [BLOCKS, N], U8)
        h_wd = [mx_tile(f"h_wd{b}", [S], U32) for b in range(BLOCKS)]
        h_sc = [mx_tile(f"h_sc{b}", [S], U8) for b in range(BLOCKS)]
        gated = [keep.tile([P, PACK, S], F32, name=f"gated{b}") for b in range(BLOCKS)]
        result = keep.tile([P, OUT_TILES * S], F32, name="result", align_bytes=DMA_ALIGN)
        ident = keep.tile([P, P], F32, name="ident")

        def load_table_words(a):
            nc.sync.dma_start(tab_wd[a][:], tab_words[a].rearrange("p t i -> p (t i)").bitcast(I32))

        def load_g(b, t, buf):
            tile = placed(f"g{b}{t}", buf * BUF, [T], F32)
            rows = gT[b * PASS : (b + 1) * PASS, :].rearrange("(p t) c -> p t c", t=PACK)
            nc.sync.dma_start(tile[:], rows[:, t, :])
            return tile

        def load_wa(b, a, buf):
            tile = placed(f"wa_raw{b}{a}", buf * BUF, [PACK, PASS], F32)
            rows = wa[a * PASS : (a + 1) * PASS, b * PASS : (b + 1) * PASS]
            nc.sync.dma_start(tile[:], rows.rearrange("(p i) c -> p i c", i=PACK))
            return tile

        def load_wc(buf):
            tile = placed("wc_raw", buf * BUF, [BLOCKS, PACK * N], F32)
            nc.sync.dma_start(tile[:], wc.rearrange("(b p t) n -> p b (t n)", b=BLOCKS, t=PACK))
            return tile

        def gather_words(a):
            nc.vector.tensor_copy(v_wd[a][:], tab_wd[a][:].bitcast(U32).indirect(offsets[:]))

        def reorder_wb(b):
            words = wb_wd_raw[:].bitcast(U16)[:, :, b * PASS : (b + 1) * PASS]
            scales = wb_sc_raw[:, :, b * PASS : (b + 1) * PASS]
            nc.scalar.copy(wb_wd[b][:].bitcast(U16), words.rearrange("p a (m t) -> p t a m", t=PACK))
            nc.vector.tensor_copy(wb_sc[b][:], scales.rearrange("p a (m t) -> p t a m", t=PACK))

        def quantize(words, scales, values):
            nc.vector.quantize_mx(out=words.bitcast(FP8X4), scales=scales, in_=values)

        def flat(tile):
            return tile[:].rearrange("p a c -> p (a c)")

        def round_wa(b, a, second=nc.scalar.copy):
            dst = wa_bf[b, a].rearrange("p (s u m i) -> p s m i u", s=2, u=2, i=PACK)
            src = wa_raw[b, a][:].rearrange("p i (m s u) -> p s m i u", s=2, u=2)
            for s, copy in enumerate((nc.scalar.copy, second)):
                copy(dst[:, s], src[:, s])
            quantize(wa_wd[b][:, a, :], wa_sc[b][:, a, :], wa_bf[b, a])

        def interleaved(ap, run=2):
            return ap.rearrange("p (c u t) -> p c t u", u=run, t=PACK)

        def by_runs(ap, run=2):
            return ap.rearrange("p t (c u) -> p c t u", u=run)

        def mx_pass(acc, n, count, lhs, lhs_sc, rhs, rhs_sc):
            nc.tensor.matmul_mx(
                out=acc, lhsT=lhs, lhsT_scale=lhs_sc, rhs=rhs.bitcast(FP8X4), rhs_scale=rhs_sc,
                start=(n == 0), stop=(n == count - 1),
            )

        def product_wb(b, t, tile, first_bank, parts=HALVES):
            for u, (lo, hi) in enumerate(parts):
                acc = bank((first_bank + u) % BANKS, [hi - lo])
                for n, a in enumerate(reversed(range(PASSES))):
                    mx_pass(acc[:], n, PASSES, wb_wd[b][:, t, a, :].bitcast(FP4X4), wb_sc[b][:, t, a, :], v_wd[a][:, lo:hi], v_sc[a][:, lo:hi])
                nc.scalar.copy(tile[:, lo:hi], acc[:])
            wb_prod[b, t] = tile

        def product_wa(acc, b, t, lo, hi):
            cols = slice(P * t, P * (t + 1))
            for a in range(PASSES):
                mx_pass(acc, a, PASSES, wa_wd[b][:, a, cols].bitcast(FP8X4), wa_sc[b][:, a, cols], v_wd[a][:, lo:hi], v_sc[a][:, lo:hi])

        def wa_in_psum(b, lo, number):
            acc = bank(number, [PACK, P])
            for t in range(PACK):
                product_wa(acc[:, t, :], b, t, lo, lo + P)
            return acc

        def wa_in_sbuf(b, lo, hi, first_bank, tile):
            share = BANK // (hi - lo)
            for first in range(0, PACK, share):
                acc = bank((first_bank + first // share) % BANKS, [share, hi - lo])
                for e in range(share):
                    product_wa(acc[:, e, :], b, first + e, lo, hi)
                for e in range(share):
                    t = first + e
                    nc.scalar.activation(tile[:, t, :], acc[:, e, :], IDENT, bias=drift_col[:, b, t : t + 1])
            return tile

        def gate(b, t, lo, hi):
            window = g_raw[b, t][:].indirect(offsets[:, lo // GROUP : hi // GROUP])
            nc.vector.tensor_tensor(gated[b][:, t, lo:hi], window, wb_prod[b, t][:, lo:hi], MULT)

        def add_drift(b, t, lo, hi):
            tile, first = drifted[b]
            nc.scalar.activation(tile[:, t, lo - first : hi - first], gated[b][:, t, lo:hi], IDENT, bias=drift_col[:, b, t : t + 1])

        def h_piece(b, lo, hi):
            h_bf[b, lo] = mx_tile(f"h_bf{b}_{lo}", [PACK * (hi - lo)], BF16)
            return h_bf[b, lo]

        def add_on_vector(b, piece, lo, acc):
            tile, first = drifted[b]
            dst = h_bf[b, piece][:, PACK * (lo - piece) : PACK * (lo - piece + P)]
            nc.vector.tensor_tensor(interleaved(dst), by_runs(acc[:]), by_runs(tile[:, :, lo - first : lo - first + P]), ADD)

        def add_from_sbuf(lo, hi):
            h_bf[1, lo] = ring.tile([P, PACK * (hi - lo)], BF16, name="h_ring", bufs=2, align_bytes=64)
            auto = autos[lo // BANK][:, :, lo % BANK : lo % BANK + hi - lo]
            nc.vector.tensor_tensor(interleaved(h_bf[1, lo][:]), by_runs(auto), by_runs(gated[1][:, :, lo:hi]), ADD)

        def add_on_gpsimd(b, lo, hi, auto):
            nc.gpsimd.tensor_tensor(interleaved(h_piece(b, lo, hi)[:], 4), by_runs(auto[:], 4), by_runs(gated[b][:, :, lo:hi], 4), ADD)

        def add_on_tensor(b, lo, auto, first_bank):
            units = range(PIECE // P)
            accs = [bank(first_bank + w, [PACK, P]) for w in units]
            for t in range(PACK):
                for w in units:
                    terms = [auto[:, t, P * w : P * (w + 1)], gated[b][:, t, lo + P * w : lo + P * (w + 1)]]
                    for n, term in enumerate(terms):
                        nc.tensor.matmul(accs[w][:, t, :], term, ident[:], start=(n == 0), stop=(n == 1), is_transpose=True)
            turned = [placed(f"turned{w}", 3 * BUF + KIB * w, [PASS], BF16) for w in units]
            for w in units:
                dst = turned[w][:].rearrange("p (u m e) -> p u m e", u=2, e=2)
                nc.scalar.copy(dst, accs[w][:].rearrange("p (u e) m -> p u m e", u=2))
            words = h_piece(b, lo, lo + PIECE)[:].bitcast(F32).rearrange("p (w j u) -> p w j u", w=2, u=2)
            acc = bank((first_bank + 2) % BANKS, [2, 2, P])
            for w in units:
                pairs = turned[w][:].bitcast(F32)
                for u in range(2):
                    nc.tensor.transpose(acc[:, w, u, :], pairs[:, P * u : P * (u + 1)], ident[:])
            nc.scalar.copy(words, acc[:].rearrange("p w u j -> p w j u"))

        def quantize_h(b, lo, hi):
            quantize(h_wd[b][:, lo:hi], h_sc[b][:, lo:hi], h_bf[b, lo][:])

        def decode(lo, hi, first_bank, last):
            piece = result[:, OUT_TILES * lo : OUT_TILES * hi].rearrange("p (c j) -> p c j", c=OUT_TILES)
            accs = [bank((first_bank + c) % BANKS, [hi - lo]) for c in range(OUT_TILES)]
            for b in range(BLOCKS):
                for c in range(OUT_TILES):
                    cols = slice(P * c, P * (c + 1))
                    mx_pass(accs[c][:], b, BLOCKS, wc_wd[:, b, cols].bitcast(FP8X4), wc_sc[:, b, cols], h_wd[b][:, lo:hi], h_sc[b][:, lo:hi])
            rows = out[:, lo:hi].rearrange("(c p) j -> p c j", p=P)
            nc.scalar.activation(piece[:, 0, :], accs[0][:], IDENT, bias=xop_col[:, 0:1])
            if last:
                nc.vector.tensor_scalar_add(piece[:, 1, :], accs[1][:], xop_col[:, 1:2])
                nc.scalar.dma_start(rows[:, 0, :], piece[:, 0, :])
                nc.sync.dma_start(rows[:, 1, :], piece[:, 1, :])
            else:
                nc.scalar.activation(piece[:, 1, :], accs[1][:], IDENT, bias=xop_col[:, 1:2])
                nc.sync.dma_start(rows, piece)

        wb_prod, h_bf, drifted = {}, {}, {}

        nc.gpsimd.memset(tab_sc[:].bitcast(I32), 0)
        make_identity(nc, ident[:])
        nc.vector.memset(wb_sc_raw[:].bitcast(I32), 0)

        load_table_words(0)
        nc.sync.dma_start(offsets[:], offs)
        for e in range(4):
            rows = tab_scales[:, e::4, :].rearrange("a q c -> q a c")
            nc.sync.dma_start(tab_sc[e:P:16, :].bitcast(I32), rows.bitcast(I32))
        nc.sync.dma_start(wb_wd_raw[:].bitcast(I32), wb_words.rearrange("a p c -> p a c").bitcast(I32))
        load_table_words(1)
        for e in range(4):
            rows = wb_scales[:, e::4, :].rearrange("a q c -> q a c")
            nc.sync.dma_start(wb_sc_raw[e:P:32, :, :].bitcast(I32), rows.bitcast(I32))
        wa_raw = {(0, a): load_wa(0, a, 2 + 2 * a) for a in range(PASSES)}
        gather_words(0)
        nc.vector.tensor_copy(v_sc[0][:], tab_sc[:].indirect(offsets[:]))
        for e in range(4):
            nc.sync.dma_start(v_sc[1][e:P:32, :].bitcast(I32), v_sc[0][16 + e : P : 32, :].bitcast(I32))
        gather_words(1)
        g_raw = {(0, 0): load_g(0, 0, 5)}
        for b in range(BLOCKS):
            reorder_wb(b)
        drift_col = placed("drift_col", 6 * BUF, [BLOCKS, PACK], F32)
        nc.sync.dma_start(drift_col[:], drift.rearrange("(b p t) -> p b t", b=BLOCKS, t=PACK))
        g_raw[0, 1] = load_g(0, 1, 1)
        g_raw[0, 2] = load_g(0, 2, 2)
        g_raw[0, 3] = load_g(0, 3, 4)

        round_wa(0, 0)
        round_wa(0, 1, nc.vector.tensor_copy)
        wa_raw[1, 0] = load_wa(1, 0, 3)
        wa_raw[1, 1] = load_wa(1, 1, 5)
        g_raw[1, 0] = load_g(1, 0, 1)
        g_raw[1, 1] = load_g(1, 1, 2)
        g_raw[1, 2] = load_g(1, 2, 4)
        early, late = keep.tile([P, 2, S], F32, name="prod_early"), placed("prod_late", 0, [2, S], F32)
        first_parts = [(0, PIECE), (PIECE, BANK), (BANK, S)]
        product_wb(0, 0, early[:, 0, :], 0, first_parts)
        for t in range(1, PACK):
            product_wb(0, t, (early, late)[t // 2][:, t % 2, :], 1 + 2 * t)
        product_wb(1, 0, keep.tile([P, S], F32, name="prod10")[:], 1)
        split = S - PIECE
        auto = wa_in_sbuf(0, split, S, BANKS - 2, keep.tile([P, PACK, PIECE], F32, name="auto0"))
        kept = [wa_in_psum(0, lo, lo // P) for lo in range(0, split, P)]
        drifted[0] = (keep.tile([P, PACK, split], F32, name="drifted0"), 0)
        for lo, hi in first_parts:
            gate(0, 0, lo, hi)
        add_drift(0, 0, 0, split)
        for t in range(1, PACK - 1):
            gate(0, t, 0, S)
            add_drift(0, t, 0, split)
        parts = [(0, split // 2), (split // 2, split)]
        for lo, hi in parts:
            gate(0, PACK - 1, lo, hi)
            add_drift(0, PACK - 1, lo, hi)
        gate(0, PACK - 1, split, S)
        for first, end in parts:
            h_piece(0, first, end)
            for lo in range(first, end, P):
                add_on_vector(0, first, lo, kept[lo // P])
        add_on_gpsimd(0, split, S, auto)
        wc_raw = load_wc(0)
        for lo, hi in (parts[0], (split, S), parts[1]):
            quantize_h(0, lo, hi)

        round_wa(1, 0)
        round_wa(1, 1)
        g_raw[1, 3] = load_g(1, 3, 7)
        middle = placed("prod_middle", 5 * BUF, [2, S], F32)
        product_wb(1, 1, middle[:, 0, :], 0)
        product_wb(1, 2, middle[:, 1, :], 2)
        product_wb(1, 3, placed("prod13", 8 * BUF, [S], F32)[:], 4)
        autos = [wa_in_sbuf(1, *HALVES[0], 6, keep.tile([P, PACK, BANK], F32, name="auto10"))]
        for b in range(BLOCKS):
            nc.scalar.copy(interleaved(wc_bf[:, b, :]), by_runs(wc_raw[:, b, :].rearrange("p (t n) -> p t n", t=PACK)))
        quantize(flat(wc_wd), flat(wc_sc), flat(wc_bf))
        autos.append(wa_in_sbuf(1, *HALVES[1], 2, placed("auto11", 0, [PACK, BANK], F32)))
        xop_col = placed("xop_col", 2 * BUF, [OUT_TILES], F32)
        with nc.allow_non_contiguous_dma(reason="one bias value a partition"):
            nc.sync.dma_start(xop_col[:], xop.rearrange("(c p) -> p c", p=P))
        for t in range(PACK - 1):
            gate(1, t, 0, S)
        for lo, hi in ((0, PIECE), (PIECE, S - PIECE), (S - PIECE, S)):
            gate(1, PACK - 1, lo, hi)
        add_on_tensor(1, 0, autos[0], 6)
        pieces = [(0, 256), (256, 512), (512, 768), (768, 896), (896, 1024)]
        add_from_sbuf(*pieces[1])
        for n, (now, later) in enumerate(((1, 2), (0, 3), (2, 4), (3, None), (4, None))):
            if later:
                add_from_sbuf(*pieces[later])
            quantize_h(1, *pieces[now])
            decode(*pieces[now], 1 + 2 * n, now == 4)
